import numpy as np
import ml_dtypes


def mxq(x, axis, fmt="e4m3"):
    dtype, down = {"e4m3": (ml_dtypes.float8_e4m3fn, 7), "e5m2": (ml_dtypes.float8_e5m2, 14)}[fmt]
    v = np.moveaxis(np.asarray(x, np.float32).astype(ml_dtypes.bfloat16).astype(np.float64), axis, -1)
    blocks = v.reshape(v.shape[:-1] + (-1, 32))
    amax = np.abs(blocks).max(-1, keepdims=True)
    byte = np.maximum(np.where(amax > 0, np.frexp(amax)[1] - 1 + 127, 0) - down, 1)
    scale = np.exp2(byte - 127.0)
    codes = (blocks / scale).astype(np.float32).astype(dtype).astype(np.float64)
    return np.moveaxis((codes * scale).reshape(v.shape), -1, axis)


WIDE = False


def mx_kscale(k):
    if not WIDE:
        return np.ones(k)
    levels = np.array([10, -10, 5, -5, 0])
    if k % 512:
        return np.exp2(np.random.permutation(np.resize(levels, k // 32))).repeat(32)
    a = np.empty((k // 512, 16))
    for p in range(k // 512):
        a[p, :8] = np.random.permutation(np.resize(levels, 8))
        for g in range(8):
            far = levels[np.abs(levels - a[p, g]) >= 10]
            a[p, g + 8] = far[np.random.randint(len(far))]
    return np.exp2(a.ravel()).repeat(32)


def f64(x):
    return np.asarray(x).astype(np.float64)


def striped(idx):
    return np.tile(np.asarray(idx).reshape(-1, 16).T, (8, 1)).astype(np.uint16)


def unstriped(offs):
    return offs[:16].T.reshape(-1).astype(np.int64)


E2M1 = np.array([0.0, 0.5, 1.0, 1.5, 2.0, 3.0, 4.0, 6.0, -0.0, -0.5, -1.0, -1.5, -2.0, -3.0, -4.0, -6.0])


def pack_weight(w, fmt):
    k, n = w.shape
    w = f64(np.asarray(w, np.float32).astype(ml_dtypes.bfloat16)).reshape(k // 32, 32, n)
    amax = np.abs(w).max(1)
    if fmt == "e4m3":
        byte = np.frexp(amax)[1] - 1 + 127 - 7
    else:
        mant, ex = np.frexp(amax / 6.0)
        byte = np.where(mant > 0.5, ex, ex - 1) + 127
    byte = np.clip(np.where(amax > 0, byte, 1), 1, 254)
    scaled = (w * np.exp2(127.0 - byte)[:, None, :]).reshape(k, n).astype(np.float32)
    by_word = np.ascontiguousarray(scaled.reshape(k // 512, 128, 4, n).transpose(0, 1, 3, 2))
    if fmt == "e4m3":
        words = by_word.astype(ml_dtypes.float8_e4m3fn).view(np.uint8)
    else:
        c = by_word.astype(ml_dtypes.float4_e2m1fn).view(np.uint8) & 0xF
        words = (c[..., 0::2] | (c[..., 1::2] << 4)).reshape(k // 512, 128, 2 * n)
    return np.ascontiguousarray(words), np.ascontiguousarray(byte.astype(np.uint8).reshape(k // 512, 16, n))


def unpack_weight(words, scales, fmt):
    g, _, n = scales.shape
    words = np.ascontiguousarray(words).reshape(g, 128, n, -1)
    if fmt == "e4m3":
        vals = words.view(ml_dtypes.float8_e4m3fn).astype(np.float64)
    else:
        nib = np.empty((g, 128, n, 4), np.uint8)
        nib[..., 0::2] = words & 0xF
        nib[..., 1::2] = words >> 4
        vals = E2M1[nib]
    vals = vals * np.repeat(np.exp2(scales.astype(np.float64) - 127.0), 8, axis=1)[..., None]
    return vals.transpose(0, 1, 3, 2).reshape(g * 512, n)


B, N, T, D, DV, NQ = 1, 1536, 4096, 1024, 128, 256
PAGE = 512


def setup_inputs():
    n = np.random.standard_normal
    pages = np.random.permutation(T // PAGE)[:B * N // PAGE]
    idx = (pages[:, None] * PAGE + np.arange(PAGE)[None, :]).reshape(-1)
    s = mx_kscale(D)[:, None]
    u = np.ones(T)
    u[idx] = mx_kscale(B * N)
    r = np.random.uniform(0.5, 2.0, T)
    k = n((D, T)) / s
    v = n((DV, T)) / (u * r)
    kp = pack_weight(k, "e2m1")
    vp = pack_weight(v.T, "e4m3")
    return {
        "qT": (n((B, D, NQ)) * s * (1.00 / np.sqrt(D))).astype(np.float32),
        "k_words": np.ascontiguousarray(kp[0].reshape(D // 1024, 2, 128, T, 2).transpose(0, 2, 3, 1, 4)).reshape(D // 1024, 128, T, 4),
        "k_scales": kp[1],
        "v_words": vp[0],
        "v_scales": vp[1],
        "vs": np.tile(u * r, (128, 1)).astype(np.float32),
        "offs": striped(idx),
        "voffs": striped((pages[:, None] * DV + np.arange(DV)[None, :]).reshape(-1)),
    }


def reference(qT, k_words, k_scales, v_words, v_scales, vs, offs, voffs):
    idx = unstriped(offs)
    k = unpack_weight(k_words.reshape(D // 1024, 128, T, 2, 2).transpose(0, 3, 1, 2, 4).reshape(D // 512, 128, 2 * T), k_scales, "e2m1")
    v = unpack_weight(v_words, v_scales, "e4m3")
    v = v.reshape(T // 512, 512, DV)[unstriped(voffs)[::DV] // DV].reshape(B, N, DV)
    pick = lambda x: x[:, idx].reshape(x.shape[0], B, N).transpose(1, 0, 2)
    q = f64(qT)
    score = mxq(q, 1, "e4m3").transpose(0, 2, 1) @ pick(k)
    p = score / (1.0 + np.exp(-score))
    w = p * pick(f64(vs))[:, :1, :]
    y = mxq(w, 2, "e4m3") @ v
    y = y / 16.0
    return y

@@ -1,0 +1,180 @@
+from contextlib import ExitStack
+
+import concourse.mybir as mybir
+from concourse.masks import make_identity
+
+N, T, D, DV, NQ = 1536, 4096, 1024, 128, 256
+PAGE = 512
+FLOPS = 2 * NQ * D * N + 2 * NQ * N * DV
+
+F32 = mybir.dt.float32
+BF16 = mybir.dt.bfloat16
+I32 = mybir.dt.int32
+U32 = mybir.dt.uint32
+U16 = mybir.dt.uint16
+U8 = mybir.dt.uint8
+FP8X4 = mybir.dt.float8_e4m3fn_x4
+FP4X4 = mybir.dt.float4_e2m1fn_x4
+ACT = mybir.ActivationFunctionType
+MULT = mybir.AluOpType.mult
+
+P = 128
+PACK = 4
+PASSES = D // (P * PACK)
+PAGES = N // PAGE
+POOL_PAGES = T // PAGE
+QBLOCKS = NQ // P
+LIST_COLS = PAGE // 16
+SHIFT = 16
+VS_ROW = 8
+
+
+def tile_attend_pkv4_silu_kernel(tc, qT, k_words, k_scales, v_words, v_scales, vs, offs, voffs, out):
+    nc = tc.nc
+    with ExitStack() as ctx:
+        keep = ctx.enter_context(tc.tile_pool(name="keep", bufs=1))
+        shared = ctx.enter_context(tc.tile_pool(name="shared", bufs=1))
+        psum = ctx.enter_context(tc.psum_pool(name="psum", bufs=1))
+
+        offs_sb = keep.tile([P, N // 16], U16, name="offs_sb")
+        nc.sync.dma_start(offs_sb[:], offs)
+        voffs_sb = keep.tile([P, PAGES * DV // 16], U16, name="voffs_sb")
+        nc.sync.dma_start(voffs_sb[:], voffs)
+
+        q_raw = keep.tile([P, PASSES, PACK * NQ], F32, name="q_raw", align_bytes=64)
+        nc.sync.dma_start(q_raw[:], qT[0].rearrange("(o p j) q -> p o (j q)", o=PASSES, j=PACK))
+        kw_pool = keep.tile([P, T], I32, name="kw_pool", align_bytes=64)
+        nc.sync.dma_start(kw_pool[:], k_words[0].rearrange("g t b -> g (t b)").bitcast(I32))
+
+        ks_pool = keep.tile([P, T // 4], I32, name="ks_pool", align_bytes=64)
+        nc.vector.memset(ks_pool[:], 0)
+        ks_rows = k_scales.bitcast(I32).rearrange("o (c r) t -> r c o t", r=4)
+        for r in range(4):
+            nc.scalar.dma_start(ks_pool[r:P:SHIFT, :], ks_rows[r])
+
+        vs_pool = shared.tile([P, T], F32, name="vs_pool", align_bytes=64, offset=0)
+        nc.vector.memset(vs_pool[:].bitcast(I32), 0)
+        nc.scalar.dma_start(vs_pool[VS_ROW : VS_ROW + 1, :], vs[0:1, :])
+
+        warm = keep.tile([P, 2], F32, name="warm", tag="warm_then_q", align_bytes=64)
+        nc.vector.memset(warm[:, 0:1], 0.0)
+        nc.scalar.activation(warm[:, 1:2], warm[:, 0:1], ACT.Silu)
+
+        ks_words = [keep.tile([P, N // 4], I32, name=f"ks_plane{o}", align_bytes=64) for o in range(PASSES)]
+        ks_plane = [plane[:].bitcast(U8) for plane in ks_words]
+        nc.vector.memset(ks_words[1][:], 0)
+        ident = keep.tile([P, P], F32, name="ident")
+        nc.vector.memset(ident[:], 0.0)
+        make_identity(nc, ident[:], nomemset=True)
+
+        q_bf = keep.tile([P, PASSES, NQ, PACK], BF16, name="q_bf", tag="warm_then_q", align_bytes=64)
+        for o in range(PASSES):
+            nc.scalar.copy(q_bf[:, o], q_raw[:, o].rearrange("p (j q) -> p q j", j=PACK))
+
+        ks_got = keep.tile([P, N], U8, name="ks_got", align_bytes=64)
+        nc.vector.tensor_copy(ks_got[:], ks_pool[:].bitcast(U8).indirect(offs_sb[:]))
+        for g in range(PAGES):
+            cols = slice(g * PAGE, (g + 1) * PAGE)
+            nc.vector.tensor_copy(
+                ks_plane[0][:, cols].rearrange("p (t s) -> p t s", t=PACK),
+                ks_got[:, cols].rearrange("p (s t) -> p t s", t=PACK),
+            )
+        nc.scalar.dma_start(ks_words[1][0 : P - SHIFT, :], ks_words[0][SHIFT:P, :])
+
+        vs_col = keep.tile([P, PAGES, PACK], F32, name="vs_col")
+        turn_tags = ["y0", "y1", "score5"]
+        for g in range(PAGES):
+            vs_got = keep.tile([P, PAGE], F32, name=f"vs_got{g}", align_bytes=64)
+            nc.vector.tensor_copy(vs_got[:], vs_pool[:].indirect(offs_sb[:, g * LIST_COLS : (g + 1) * LIST_COLS]))
+            turned = psum.tile([P, PACK, P], F32, name=f"turned{g}", tag=turn_tags[g])
+            for t in range(PACK):
+                nc.tensor.transpose(turned[:, t, :], vs_got[:, t:PAGE:PACK], ident[:])
+            nc.scalar.copy(vs_col[:, g, :], turned[:, :, VS_ROW])
+
+        vw_pool = shared.tile([P, POOL_PAGES * DV], I32, name="vw_pool", align_bytes=64, offset=0)
+        nc.sync.dma_start(
+            vw_pool[:].rearrange("g (u e) -> g u e", u=POOL_PAGES),
+            v_words.rearrange("u g e r -> g u (e r)").bitcast(I32),
+        )
+        vsc_pool = shared.tile([P, POOL_PAGES * DV // 4], I32, name="vsc_pool", align_bytes=64, offset=4096)
+        nc.vector.memset(vsc_pool[:], 0)
+        vsc_rows = v_scales.bitcast(I32).rearrange("u f e -> f u e")
+        for c in range(4):
+            nc.sync.dma_start(
+                vsc_pool[32 * c : 32 * c + 4, :].rearrange("f (u e) -> f u e", u=POOL_PAGES),
+                vsc_rows[4 * c : 4 * c + 4],
+            )
+
+        q_codes = shared.tile([P, PASSES, NQ], U32, name="q_codes", align_bytes=64, offset=5120)
+        q_scales = shared.tile([P, PASSES, NQ], U8, name="q_scales", align_bytes=64, offset=7168)
+        nc.vector.quantize_mx(
+            out=q_codes[:].rearrange("p o q -> p (o q)").bitcast(FP8X4),
+            scales=q_scales[:].rearrange("p o q -> p (o q)"),
+            in_=q_bf[:].rearrange("p o q j -> p (o q j)"),
+        )
+
+        weights = []
+        for g in range(PAGES):
+            kw_got = shared.tile([P, PAGE], U32, name=f"kw_got{g}", align_bytes=64, offset=8192 + 2048 * g)
+            nc.vector.tensor_copy(kw_got[:], kw_pool[:].bitcast(U32).indirect(offs_sb[:, g * LIST_COLS : (g + 1) * LIST_COLS]))
+            keys = keep.tile([P, PASSES, 2 * PAGE], U8, name=f"keys{g}", align_bytes=64)
+            halves = kw_got[:].bitcast(U16).rearrange("p (s t o) -> p o s t", t=PACK, o=PASSES)
+            for o in range(PASSES):
+                nc.vector.tensor_copy(keys[:, o, :].bitcast(U16).rearrange("p (t s) -> p s t", t=PACK), halves[:, o])
+            for b in range(QBLOCKS):
+                score = psum.tile([P, PACK, P], F32, name=f"score{g}_{b}", tag=f"score{g * QBLOCKS + b}")
+                for t in range(PACK):
+                    for o in range(PASSES):
+                        nc.tensor.matmul_mx(
+                            out=score[:, t, :],
+                            lhsT=keys[:, o, 2 * P * t : 2 * P * (t + 1)].bitcast(FP4X4),
+                            lhsT_scale=ks_plane[o][:, g * PAGE + P * t : g * PAGE + P * (t + 1)],
+                            rhs=q_codes[:, o, b * P : (b + 1) * P].bitcast(FP8X4),
+                            rhs_scale=q_scales[:, o, b * P : (b + 1) * P],
+                            start=(o == 0),
+                            stop=(o == PASSES - 1),
+                        )
+                silu = keep.tile([P, P, PACK], F32, name=f"silu{g}_{b}", align_bytes=64)
+                nc.scalar.activation(silu[:], score[:].rearrange("p t q -> p q t"), ACT.Silu)
+                weights.append((g, b, silu))
+
+        vw_got = keep.tile([P, PAGES * DV], U32, name="vw_got", align_bytes=64)
+        nc.vector.tensor_copy(vw_got[:], vw_pool[:].bitcast(U32).indirect(voffs_sb[:]))
+        vsc_got = keep.tile([P, PAGES * DV], U8, name="vsc_got", align_bytes=64)
+        nc.vector.tensor_copy(vsc_got[:], vsc_pool[:].bitcast(U8).indirect(voffs_sb[:]))
+
+        y = [psum.tile([P, DV], F32, name=f"y{b}", tag=f"y{b}") for b in range(QBLOCKS)]
+
+        def scale(g, b, silu):
+            w_bf = keep.tile([P, P, PACK], BF16, name=f"w_bf{g}_{b}", align_bytes=64)
+            nc.vector.tensor_tensor(w_bf[:], silu[:], vs_col[:, g, :].unsqueeze(1).to_broadcast([P, P, PACK]), MULT)
+            return w_bf
+
+        def multiply(g, b, w_bf):
+            w_codes = keep.tile([P, P], U32, name=f"w_codes{g}_{b}", align_bytes=64)
+            w_scales = keep.tile([P, P], U8, name=f"w_scales{g}_{b}", align_bytes=64)
+            nc.vector.quantize_mx(
+                out=w_codes[:].bitcast(FP8X4), scales=w_scales[:], in_=w_bf[:].rearrange("p q t -> p (q t)")
+            )
+            nc.tensor.matmul_mx(
+                out=y[b][:],
+                lhsT=w_codes[:].bitcast(FP8X4),
+                lhsT_scale=w_scales[:],
+                rhs=vw_got[:, g * DV : (g + 1) * DV].bitcast(FP8X4),
+                rhs_scale=vsc_got[:, g * DV : (g + 1) * DV],
+                start=(g == 0),
+                stop=(g == PAGES - 1),
+            )
+            if g == PAGES - 1:
+                result = keep.tile([P, DV], F32, name=f"result{b}")
+                nc.scalar.activation(result[:], y[b][:], ACT.Copy, scale=1.0 / 16.0)
+                queue = nc.sync if b == 0 else nc.scalar
+                queue.dma_start(out[0, b * P : (b + 1) * P, :], result[:])
+
+        pending = None
+        for g, b, silu in weights:
+            w_bf = scale(g, b, silu)
+            if pending is not None:
+                multiply(*pending)
+            pending = (g, b, w_bf)
+        multiply(*pending)

@@ -25,8 +25,11 @@ PAGES = N // PAGE
 POOL_PAGES = T // PAGE
 QBLOCKS = NQ // P
 LIST_COLS = PAGE // 16
-SHIFT = 16
 VS_ROW = 8
+VS_AT = 4 * T + 2 * PASSES * NQ * PACK
+GOT_AT = VS_AT + 4 * T
+WARM_PASSES = 3
+SCORE_BANKS = 4
 
 
 def tile_attend_pkv4_silu_kernel(tc, qT, k_words, k_scales, v_words, v_scales, vs, offs, voffs, out):
@@ -38,65 +41,19 @@ def tile_attend_pkv4_silu_kernel(tc, qT, k_words, k_scales, v_words, v_scales, v
 
         offs_sb = keep.tile([P, N // 16], U16, name="offs_sb")
         nc.sync.dma_start(offs_sb[:], offs)
+        ks_pool = keep.tile([P, T // 4], I32, name="ks_pool", align_bytes=64)
+        ks_rows = k_scales.bitcast(I32).rearrange("o f t -> (o f) t")
+        nc.sync.dma_start(ks_pool[0:32, :], ks_rows)
+        nc.sync.dma_start(ks_pool[32:48, :], ks_rows[4:20])
+        nc.sync.dma_start(ks_pool[48:64, :], ks_rows[16:32])
+        q_raw = keep.tile([P, PASSES, PACK * NQ], F32, name="q_raw", align_bytes=64)
+        q_rows = qT[0].rearrange("(o p j) q -> o p (j q)", o=PASSES, j=PACK)
+        for o in range(PASSES):
+            nc.sync.dma_start(q_raw[:, o], q_rows[o])
         voffs_sb = keep.tile([P, PAGES * DV // 16], U16, name="voffs_sb")
         nc.sync.dma_start(voffs_sb[:], voffs)
 
-        q_raw = keep.tile([P, PASSES, PACK * NQ], F32, name="q_raw", align_bytes=64)
-        nc.sync.dma_start(q_raw[:], qT[0].rearrange("(o p j) q -> p o (j q)", o=PASSES, j=PACK))
-        kw_pool = keep.tile([P, T], I32, name="kw_pool", align_bytes=64)
-        nc.sync.dma_start(kw_pool[:], k_words[0].rearrange("g t b -> g (t b)").bitcast(I32))
-
-        ks_pool = keep.tile([P, T // 4], I32, name="ks_pool", align_bytes=64)
-        nc.vector.memset(ks_pool[:], 0)
-        ks_rows = k_scales.bitcast(I32).rearrange("o (c r) t -> r c o t", r=4)
-        for r in range(4):
-            nc.scalar.dma_start(ks_pool[r:P:SHIFT, :], ks_rows[r])
-
-        vs_pool = shared.tile([P, T], F32, name="vs_pool", align_bytes=64, offset=0)
-        nc.vector.memset(vs_pool[:].bitcast(I32), 0)
-        nc.scalar.dma_start(vs_pool[VS_ROW : VS_ROW + 1, :], vs[0:1, :])
-
-        warm = keep.tile([P, 2], F32, name="warm", tag="warm_then_q", align_bytes=64)
-        nc.vector.memset(warm[:, 0:1], 0.0)
-        nc.scalar.activation(warm[:, 1:2], warm[:, 0:1], ACT.Silu)
-
-        ks_words = [keep.tile([P, N // 4], I32, name=f"ks_plane{o}", align_bytes=64) for o in range(PASSES)]
-        ks_plane = [plane[:].bitcast(U8) for plane in ks_words]
-        nc.vector.memset(ks_words[1][:], 0)
-        ident = keep.tile([P, P], F32, name="ident")
-        nc.vector.memset(ident[:], 0.0)
-        make_identity(nc, ident[:], nomemset=True)
-
-        q_bf = keep.tile([P, PASSES, NQ, PACK], BF16, name="q_bf", tag="warm_then_q", align_bytes=64)
-        for o in range(PASSES):
-            nc.scalar.copy(q_bf[:, o], q_raw[:, o].rearrange("p (j q) -> p q j", j=PACK))
-
-        ks_got = keep.tile([P, N], U8, name="ks_got", align_bytes=64)
-        nc.vector.tensor_copy(ks_got[:], ks_pool[:].bitcast(U8).indirect(offs_sb[:]))
-        for g in range(PAGES):
-            cols = slice(g * PAGE, (g + 1) * PAGE)
-            nc.vector.tensor_copy(
-                ks_plane[0][:, cols].rearrange("p (t s) -> p t s", t=PACK),
-                ks_got[:, cols].rearrange("p (s t) -> p t s", t=PACK),
-            )
-        nc.scalar.dma_start(ks_words[1][0 : P - SHIFT, :], ks_words[0][SHIFT:P, :])
-
-        vs_col = keep.tile([P, PAGES, PACK], F32, name="vs_col")
-        turn_tags = ["y0", "y1", "score5"]
-        for g in range(PAGES):
-            vs_got = keep.tile([P, PAGE], F32, name=f"vs_got{g}", align_bytes=64)
-            nc.vector.tensor_copy(vs_got[:], vs_pool[:].indirect(offs_sb[:, g * LIST_COLS : (g + 1) * LIST_COLS]))
-            turned = psum.tile([P, PACK, P], F32, name=f"turned{g}", tag=turn_tags[g])
-            for t in range(PACK):
-                nc.tensor.transpose(turned[:, t, :], vs_got[:, t:PAGE:PACK], ident[:])
-            nc.scalar.copy(vs_col[:, g, :], turned[:, :, VS_ROW])
-
-        vw_pool = shared.tile([P, POOL_PAGES * DV], I32, name="vw_pool", align_bytes=64, offset=0)
-        nc.sync.dma_start(
-            vw_pool[:].rearrange("g (u e) -> g u e", u=POOL_PAGES),
-            v_words.rearrange("u g e r -> g u (e r)").bitcast(I32),
-        )
-        vsc_pool = shared.tile([P, POOL_PAGES * DV // 4], I32, name="vsc_pool", align_bytes=64, offset=4096)
+        vsc_pool = keep.tile([P, POOL_PAGES * DV // 4], I32, name="vsc_pool", align_bytes=64)
         nc.vector.memset(vsc_pool[:], 0)
         vsc_rows = v_scales.bitcast(I32).rearrange("u f e -> f u e")
         for c in range(4):
@@ -105,24 +62,87 @@ def tile_attend_pkv4_silu_kernel(tc, qT, k_words, k_scales, v_words, v_scales, v
                 vsc_rows[4 * c : 4 * c + 4],
             )
 
-        q_codes = shared.tile([P, PASSES, NQ], U32, name="q_codes", align_bytes=64, offset=5120)
-        q_scales = shared.tile([P, PASSES, NQ], U8, name="q_scales", align_bytes=64, offset=7168)
+        vs_pool = shared.tile([P, T], F32, name="vs_pool", align_bytes=64, offset=VS_AT)
+        nc.vector.memset(vs_pool[:].bitcast(I32), 0)
+        nc.sync.dma_start(vs_pool[VS_ROW : VS_ROW + 1, :], vs[0:1, :])
+
+        warm = shared.tile([P, 32], F32, name="warm", align_bytes=64, offset=4 * T - 64)
+        nc.vector.memset(warm[:, 0:1], 0.0)
+        nc.scalar.activation(warm[:, 16:17], warm[:, 0:1], ACT.Silu)
+        kw_pool = shared.tile([P, T], I32, name="kw_pool", align_bytes=64, offset=0)
+        nc.sync.dma_start(kw_pool[:], k_words[0].rearrange("g t b -> g (t b)").bitcast(I32))
+
+        nc.vector.memset(ks_pool[64:P, :], 0)
+
+        q_bf = shared.tile([P, PASSES, NQ, PACK], BF16, name="q_bf", align_bytes=64, offset=4 * T)
+        for o in range(PASSES):
+            nc.scalar.copy(q_bf[:, o], q_raw[:, o].rearrange("p (j q) -> p q j", j=PACK))
+
+        ks_words = [keep.tile([P, N // 4], I32, name=f"ks_plane{o}", align_bytes=64) for o in range(PASSES)]
+        ks_plane = [plane[:].bitcast(U8) for plane in ks_words]
+        ks_got = keep.tile([P, N], U8, name="ks_got", tag="scales_then_values", align_bytes=64)
+        nc.vector.tensor_copy(ks_got[:], ks_pool[:].bitcast(U8).indirect(offs_sb[:]))
+        nc.vector.memset(ks_words[1][:], 0)
+        for g in range(PAGES):
+            cols = slice(g * PAGE, (g + 1) * PAGE)
+            nc.vector.tensor_copy(
+                ks_plane[0][:, cols].rearrange("p (t s) -> p t s", t=PACK),
+                ks_got[:, cols].rearrange("p (s t) -> p t s", t=PACK),
+            )
+        for o in range(PASSES):
+            for c in range(4):
+                if o > 0 or c > 1:
+                    row = 16 * o + 4 * c
+                    nc.sync.dma_start(ks_words[o][32 * c : 32 * c + 4, :], ks_words[0][row : row + 4, :])
+        vw_pool = keep.tile([P, POOL_PAGES * DV], I32, name="vw_pool", tag="scales_then_values", align_bytes=64)
+        nc.sync.dma_start(
+            vw_pool[:].rearrange("g (u e) -> g u e", u=POOL_PAGES),
+            v_words.rearrange("u g e r -> g u (e r)").bitcast(I32),
+        )
+
+        ident = keep.tile([P, P], F32, name="ident")
+        nc.vector.memset(ident[:], 0.0)
+        make_identity(nc, ident[:], nomemset=True)
+
+        vs_col = keep.tile([P, PAGES, PACK], F32, name="vs_col")
+        vs_got = keep.tile([P, PAGES, PAGE], F32, name="vs_got", align_bytes=64)
+        for g in range(PAGES):
+            nc.vector.tensor_copy(vs_got[:, g, :], vs_pool[:].indirect(offs_sb[:, g * LIST_COLS : (g + 1) * LIST_COLS]))
+            turned = psum.tile([P, PACK, P], F32, name=f"turned{g}")
+            for t in range(PACK):
+                nc.tensor.transpose(turned[:, t, :], vs_got[:, g, t:PAGE:PACK], ident[:])
+            nc.scalar.copy(vs_col[:, g, :], turned[:, :, VS_ROW])
+
+        q_codes = shared.tile([P, PASSES, NQ], U32, name="q_codes", align_bytes=64, offset=VS_AT)
+        q_scales = keep.tile([P, PASSES, NQ], U8, name="q_scales", align_bytes=64)
         nc.vector.quantize_mx(
             out=q_codes[:].rearrange("p o q -> p (o q)").bitcast(FP8X4),
             scales=q_scales[:].rearrange("p o q -> p (o q)"),
             in_=q_bf[:].rearrange("p o q j -> p (o q j)"),
         )
 
+        idle = psum.tile([P, PASSES * NQ], F32, name="idle", tag="turned0")
+        for repeat in range(WARM_PASSES):
+            nc.tensor.matmul_mx(
+                out=idle[:],
+                lhsT=q_codes[:, 0, 0:P].bitcast(FP8X4),
+                lhsT_scale=q_scales[:, 0, 0:P],
+                rhs=q_codes[:].rearrange("p o q -> p (o q)").bitcast(FP8X4),
+                rhs_scale=q_scales[:].rearrange("p o q -> p (o q)"),
+                start=True,
+                stop=True,
+            )
+
         weights = []
         for g in range(PAGES):
-            kw_got = shared.tile([P, PAGE], U32, name=f"kw_got{g}", align_bytes=64, offset=8192 + 2048 * g)
+            kw_got = shared.tile([P, PAGE], U32, name=f"kw_got{g}", align_bytes=64, offset=GOT_AT + 4 * PAGE * (g % 2))
             nc.vector.tensor_copy(kw_got[:], kw_pool[:].bitcast(U32).indirect(offs_sb[:, g * LIST_COLS : (g + 1) * LIST_COLS]))
             keys = keep.tile([P, PASSES, 2 * PAGE], U8, name=f"keys{g}", align_bytes=64)
             halves = kw_got[:].bitcast(U16).rearrange("p (s t o) -> p o s t", t=PACK, o=PASSES)
             for o in range(PASSES):
                 nc.vector.tensor_copy(keys[:, o, :].bitcast(U16).rearrange("p (t s) -> p s t", t=PACK), halves[:, o])
             for b in range(QBLOCKS):
-                score = psum.tile([P, PACK, P], F32, name=f"score{g}_{b}", tag=f"score{g * QBLOCKS + b}")
+                score = psum.tile([P, PACK, P], F32, name=f"score{g}_{b}", tag=f"score{(g * QBLOCKS + b) % SCORE_BANKS}")
                 for t in range(PACK):
                     for o in range(PASSES):
                         nc.tensor.matmul_mx(
@@ -138,12 +158,12 @@ def tile_attend_pkv4_silu_kernel(tc, qT, k_words, k_scales, v_words, v_scales, v
                 nc.scalar.activation(silu[:], score[:].rearrange("p t q -> p q t"), ACT.Silu)
                 weights.append((g, b, silu))
 
-        vw_got = keep.tile([P, PAGES * DV], U32, name="vw_got", align_bytes=64)
+        vw_got = shared.tile([P, PAGES * DV], U32, name="vw_got", align_bytes=64, offset=GOT_AT + 4 * PAGE)
         nc.vector.tensor_copy(vw_got[:], vw_pool[:].bitcast(U32).indirect(voffs_sb[:]))
-        vsc_got = keep.tile([P, PAGES * DV], U8, name="vsc_got", align_bytes=64)
+        vsc_got = shared.tile([P, PAGES * DV], U8, name="vsc_got", align_bytes=64, offset=GOT_AT + 4 * PAGE + 4 * PAGES * DV)
         nc.vector.tensor_copy(vsc_got[:], vsc_pool[:].bitcast(U8).indirect(voffs_sb[:]))
 
-        y = [psum.tile([P, DV], F32, name=f"y{b}", tag=f"y{b}") for b in range(QBLOCKS)]
+        y = [psum.tile([P, DV], F32, name=f"y{b}", tag=f"score{((PAGES - 1) * QBLOCKS + b) % SCORE_BANKS}") for b in range(QBLOCKS)]
 
         def scale(g, b, silu):
             w_bf = keep.tile([P, P, PACK], BF16, name=f"w_bf{g}_{b}", align_bytes=64)

@@ -25,7 +25,7 @@ PAGES = N // PAGE
 POOL_PAGES = T // PAGE
 QBLOCKS = NQ // P
 LIST_COLS = PAGE // 16
-VS_ROW = 8
+VS_ROW = 72
 VS_AT = 4 * T + 2 * PASSES * NQ * PACK
 GOT_AT = VS_AT + 4 * T
 WARM_PASSES = 3
@@ -41,6 +41,8 @@ def tile_attend_pkv4_silu_kernel(tc, qT, k_words, k_scales, v_words, v_scales, v
 
         offs_sb = keep.tile([P, N // 16], U16, name="offs_sb")
         nc.sync.dma_start(offs_sb[:], offs)
+        voffs_sb = keep.tile([P, PAGES * DV // 16], U16, name="voffs_sb")
+        nc.sync.dma_start(voffs_sb[:], voffs)
         ks_pool = keep.tile([P, T // 4], I32, name="ks_pool", align_bytes=64)
         ks_rows = k_scales.bitcast(I32).rearrange("o f t -> (o f) t")
         nc.sync.dma_start(ks_pool[0:32, :], ks_rows)
@@ -50,8 +52,6 @@ def tile_attend_pkv4_silu_kernel(tc, qT, k_words, k_scales, v_words, v_scales, v
         q_rows = qT[0].rearrange("(o p j) q -> o p (j q)", o=PASSES, j=PACK)
         for o in range(PASSES):
             nc.sync.dma_start(q_raw[:, o], q_rows[o])
-        voffs_sb = keep.tile([P, PAGES * DV // 16], U16, name="voffs_sb")
-        nc.sync.dma_start(voffs_sb[:], voffs)
 
         vsc_pool = keep.tile([P, POOL_PAGES * DV // 4], I32, name="vsc_pool", align_bytes=64)
         nc.vector.memset(vsc_pool[:], 0)
@@ -138,9 +138,9 @@ def tile_attend_pkv4_silu_kernel(tc, qT, k_words, k_scales, v_words, v_scales, v
             kw_got = shared.tile([P, PAGE], U32, name=f"kw_got{g}", align_bytes=64, offset=GOT_AT + 4 * PAGE * (g % 2))
             nc.vector.tensor_copy(kw_got[:], kw_pool[:].bitcast(U32).indirect(offs_sb[:, g * LIST_COLS : (g + 1) * LIST_COLS]))
             keys = keep.tile([P, PASSES, 2 * PAGE], U8, name=f"keys{g}", align_bytes=64)
-            halves = kw_got[:].bitcast(U16).rearrange("p (s t o) -> p o s t", t=PACK, o=PASSES)
+            halves = kw_got[:].bitcast(U16).rearrange("p (c i t o) -> p o c t i", i=4, t=PACK, o=PASSES)
             for o in range(PASSES):
-                nc.vector.tensor_copy(keys[:, o, :].bitcast(U16).rearrange("p (t s) -> p s t", t=PACK), halves[:, o])
+                nc.vector.tensor_copy(keys[:, o, :].bitcast(U16).rearrange("p (t c i) -> p c t i", t=PACK, i=4), halves[:, o])
             for b in range(QBLOCKS):
                 score = psum.tile([P, PACK, P], F32, name=f"score{g}_{b}", tag=f"score{(g * QBLOCKS + b) % SCORE_BANKS}")
                 for t in range(PACK):

@@ -54,7 +54,7 @@ def tile_attend_pkv4_silu_kernel(tc, qT, k_words, k_scales, v_words, v_scales, v
             nc.sync.dma_start(q_raw[:, o], q_rows[o])
 
         vsc_pool = keep.tile([P, POOL_PAGES * DV // 4], I32, name="vsc_pool", align_bytes=64)
-        nc.vector.memset(vsc_pool[:], 0)
+        nc.gpsimd.memset(vsc_pool[:], 0)
         vsc_rows = v_scales.bitcast(I32).rearrange("u f e -> f u e")
         for c in range(4):
             nc.sync.dma_start(
@@ -83,12 +83,10 @@ def tile_attend_pkv4_silu_kernel(tc, qT, k_words, k_scales, v_words, v_scales, v
         ks_got = keep.tile([P, N], U8, name="ks_got", tag="scales_then_values", align_bytes=64)
         nc.vector.tensor_copy(ks_got[:], ks_pool[:].bitcast(U8).indirect(offs_sb[:]))
         nc.vector.memset(ks_words[1][:], 0)
-        for g in range(PAGES):
-            cols = slice(g * PAGE, (g + 1) * PAGE)
-            nc.vector.tensor_copy(
-                ks_plane[0][:, cols].rearrange("p (t s) -> p t s", t=PACK),
-                ks_got[:, cols].rearrange("p (s t) -> p t s", t=PACK),
-            )
+        nc.vector.tensor_copy(
+            ks_plane[0].rearrange("p (g h t s) -> p h g t s", g=PAGES, h=2, t=PACK // 2),
+            ks_got[:].rearrange("p (g s h t) -> p h g t s", g=PAGES, h=2, t=PACK // 2),
+        )
         for o in range(PASSES):
             for c in range(4):
                 if o > 0 or c > 1:
@@ -101,8 +99,7 @@ def tile_attend_pkv4_silu_kernel(tc, qT, k_words, k_scales, v_words, v_scales, v
         )
 
         ident = keep.tile([P, P], F32, name="ident")
-        nc.vector.memset(ident[:], 0.0)
-        make_identity(nc, ident[:], nomemset=True)
+        make_identity(nc, ident[:])
 
         vs_col = keep.tile([P, PAGES, PACK], F32, name="vs_col")
         vs_got = keep.tile([P, PAGES, PAGE], F32, name="vs_got", align_bytes=64)
@@ -112,6 +109,9 @@ def tile_attend_pkv4_silu_kernel(tc, qT, k_words, k_scales, v_words, v_scales, v
             for t in range(PACK):
                 nc.tensor.transpose(turned[:, t, :], vs_got[:, g, t:PAGE:PACK], ident[:])
             nc.scalar.copy(vs_col[:, g, :], turned[:, :, VS_ROW])
+
+        vsc_got = keep.tile([P, PAGES * DV], U8, name="vsc_got", align_bytes=64)
+        nc.vector.tensor_copy(vsc_got[:], vsc_pool[:].bitcast(U8).indirect(voffs_sb[:]))
 
         q_codes = shared.tile([P, PASSES, NQ], U32, name="q_codes", align_bytes=64, offset=VS_AT)
         q_scales = keep.tile([P, PASSES, NQ], U8, name="q_scales", align_bytes=64)
@@ -160,8 +160,6 @@ def tile_attend_pkv4_silu_kernel(tc, qT, k_words, k_scales, v_words, v_scales, v
 
         vw_got = shared.tile([P, PAGES * DV], U32, name="vw_got", align_bytes=64, offset=GOT_AT + 4 * PAGE)
         nc.vector.tensor_copy(vw_got[:], vw_pool[:].bitcast(U32).indirect(voffs_sb[:]))
-        vsc_got = shared.tile([P, PAGES * DV], U8, name="vsc_got", align_bytes=64, offset=GOT_AT + 4 * PAGE + 4 * PAGES * DV)
-        nc.vector.tensor_copy(vsc_got[:], vsc_pool[:].bitcast(U8).indirect(voffs_sb[:]))
 
         y = [psum.tile([P, DV], F32, name=f"y{b}", tag=f"score{((PAGES - 1) * QBLOCKS + b) % SCORE_BANKS}") for b in range(QBLOCKS)]
 

@@ -1,7 +1,6 @@
 from contextlib import ExitStack
 
 import concourse.mybir as mybir
-from concourse.masks import make_identity
 
 N, T, D, DV, NQ = 1536, 4096, 1024, 128, 256
 PAGE = 512
@@ -25,10 +24,10 @@ PAGES = N // PAGE
 POOL_PAGES = T // PAGE
 QBLOCKS = NQ // P
 LIST_COLS = PAGE // 16
-VS_ROW = 72
+VS_ROW = 8
+KS_ROW = 96
 VS_AT = 4 * T + 2 * PASSES * NQ * PACK
 GOT_AT = VS_AT + 4 * T
-WARM_PASSES = 3
 SCORE_BANKS = 4
 
 
@@ -44,10 +43,8 @@ def tile_attend_pkv4_silu_kernel(tc, qT, k_words, k_scales, v_words, v_scales, v
         voffs_sb = keep.tile([P, PAGES * DV // 16], U16, name="voffs_sb")
         nc.sync.dma_start(voffs_sb[:], voffs)
         ks_pool = keep.tile([P, T // 4], I32, name="ks_pool", align_bytes=64)
-        ks_rows = k_scales.bitcast(I32).rearrange("o f t -> (o f) t")
-        nc.sync.dma_start(ks_pool[0:32, :], ks_rows)
-        nc.sync.dma_start(ks_pool[32:48, :], ks_rows[4:20])
-        nc.sync.dma_start(ks_pool[48:64, :], ks_rows[16:32])
+        for o in range(PASSES):
+            nc.sync.dma_start(ks_pool[KS_ROW + o : P : PASSES, :], k_scales.bitcast(I32)[o])
         q_raw = keep.tile([P, PASSES, PACK * NQ], F32, name="q_raw", align_bytes=64)
         q_rows = qT[0].rearrange("(o p j) q -> o p (j q)", o=PASSES, j=PACK)
         for o in range(PASSES):
@@ -72,43 +69,37 @@ def tile_attend_pkv4_silu_kernel(tc, qT, k_words, k_scales, v_words, v_scales, v
         kw_pool = shared.tile([P, T], I32, name="kw_pool", align_bytes=64, offset=0)
         nc.sync.dma_start(kw_pool[:], k_words[0].rearrange("g t b -> g (t b)").bitcast(I32))
 
-        nc.vector.memset(ks_pool[64:P, :], 0)
+        nc.vector.memset(ks_pool[0:KS_ROW, :], 0)
 
         q_bf = shared.tile([P, PASSES, NQ, PACK], BF16, name="q_bf", align_bytes=64, offset=4 * T)
         for o in range(PASSES):
             nc.scalar.copy(q_bf[:, o], q_raw[:, o].rearrange("p (j q) -> p q j", j=PACK))
 
-        ks_words = [keep.tile([P, N // 4], I32, name=f"ks_plane{o}", align_bytes=64) for o in range(PASSES)]
-        ks_plane = [plane[:].bitcast(U8) for plane in ks_words]
+        ks_words = keep.tile([P, PASSES * N // 4], I32, name="ks_words", align_bytes=64)
+        nc.gpsimd.memset(ks_words[:], 0)
+        ks_plane = [ks_words[:].bitcast(U8)[:, o * N : (o + 1) * N] for o in range(PASSES)]
         ks_got = keep.tile([P, N], U8, name="ks_got", tag="scales_then_values", align_bytes=64)
         nc.vector.tensor_copy(ks_got[:], ks_pool[:].bitcast(U8).indirect(offs_sb[:]))
-        nc.vector.memset(ks_words[1][:], 0)
+        ks_dealt = keep.tile([P, N // 4], I32, name="ks_dealt", align_bytes=64)
         nc.vector.tensor_copy(
-            ks_plane[0].rearrange("p (g h t s) -> p h g t s", g=PAGES, h=2, t=PACK // 2),
+            ks_dealt[:].bitcast(U8).rearrange("p (g h t s) -> p h g t s", g=PAGES, h=2, t=PACK // 2),
             ks_got[:].rearrange("p (g s h t) -> p h g t s", g=PAGES, h=2, t=PACK // 2),
         )
-        for o in range(PASSES):
-            for c in range(4):
-                if o > 0 or c > 1:
-                    row = 16 * o + 4 * c
-                    nc.sync.dma_start(ks_words[o][32 * c : 32 * c + 4, :], ks_words[0][row : row + 4, :])
+        for c in range(4):
+            nc.sync.dma_start(ks_words[32 * c : 32 * c + 4, :], ks_dealt[KS_ROW + 8 * c : KS_ROW + 8 * c + 8, :])
         vw_pool = keep.tile([P, POOL_PAGES * DV], I32, name="vw_pool", tag="scales_then_values", align_bytes=64)
         nc.sync.dma_start(
             vw_pool[:].rearrange("g (u e) -> g u e", u=POOL_PAGES),
             v_words.rearrange("u g e r -> g u (e r)").bitcast(I32),
         )
 
-        ident = keep.tile([P, P], F32, name="ident")
-        make_identity(nc, ident[:])
-
-        vs_col = keep.tile([P, PAGES, PACK], F32, name="vs_col")
-        vs_got = keep.tile([P, PAGES, PAGE], F32, name="vs_got", align_bytes=64)
+        vs_got = keep.tile([P, N], F32, name="vs_got", align_bytes=64)
+        nc.vector.tensor_copy(vs_got[:], vs_pool[:].indirect(offs_sb[:]))
+        vs_col = []
         for g in range(PAGES):
-            nc.vector.tensor_copy(vs_got[:, g, :], vs_pool[:].indirect(offs_sb[:, g * LIST_COLS : (g + 1) * LIST_COLS]))
-            turned = psum.tile([P, PACK, P], F32, name=f"turned{g}")
-            for t in range(PACK):
-                nc.tensor.transpose(turned[:, t, :], vs_got[:, g, t:PAGE:PACK], ident[:])
-            nc.scalar.copy(vs_col[:, g, :], turned[:, :, VS_ROW])
+            col = keep.tile([P, PACK], F32, name=f"vs_col{g}")
+            nc.sync.dma_start(col[:], vs_got[VS_ROW : VS_ROW + 1, g * PAGE : (g + 1) * PAGE])
+            vs_col.append(col)
 
         vsc_got = keep.tile([P, PAGES * DV], U8, name="vsc_got", align_bytes=64)
         nc.vector.tensor_copy(vsc_got[:], vsc_pool[:].bitcast(U8).indirect(voffs_sb[:]))
@@ -120,18 +111,6 @@ def tile_attend_pkv4_silu_kernel(tc, qT, k_words, k_scales, v_words, v_scales, v
             scales=q_scales[:].rearrange("p o q -> p (o q)"),
             in_=q_bf[:].rearrange("p o q j -> p (o q j)"),
         )
-
-        idle = psum.tile([P, PASSES * NQ], F32, name="idle", tag="turned0")
-        for repeat in range(WARM_PASSES):
-            nc.tensor.matmul_mx(
-                out=idle[:],
-                lhsT=q_codes[:, 0, 0:P].bitcast(FP8X4),
-                lhsT_scale=q_scales[:, 0, 0:P],
-                rhs=q_codes[:].rearrange("p o q -> p (o q)").bitcast(FP8X4),
-                rhs_scale=q_scales[:].rearrange("p o q -> p (o q)"),
-                start=True,
-                stop=True,
-            )
 
         weights = []
         for g in range(PAGES):
@@ -165,7 +144,7 @@ def tile_attend_pkv4_silu_kernel(tc, qT, k_words, k_scales, v_words, v_scales, v
 
         def scale(g, b, silu):
             w_bf = keep.tile([P, P, PACK], BF16, name=f"w_bf{g}_{b}", align_bytes=64)
-            nc.vector.tensor_tensor(w_bf[:], silu[:], vs_col[:, g, :].unsqueeze(1).to_broadcast([P, P, PACK]), MULT)
+            nc.vector.tensor_tensor(w_bf[:], silu[:], vs_col[g][:].unsqueeze(1).to_broadcast([P, P, PACK]), MULT)
             return w_bf
 
         def multiply(g, b, w_bf):

@@ -65,7 +65,8 @@ def tile_attend_pkv4_silu_kernel(tc, qT, k_words, k_scales, v_words, v_scales, v
 
         warm = shared.tile([P, 32], F32, name="warm", align_bytes=64, offset=4 * T - 64)
         nc.vector.memset(warm[:, 0:1], 0.0)
-        nc.scalar.activation(warm[:, 16:17], warm[:, 0:1], ACT.Silu)
+        warmed = keep.tile([P, 1], F32, name="warmed", tag="planes", align_bytes=64)
+        nc.scalar.activation(warmed[:], warm[:, 0:1], ACT.Silu)
         kw_pool = shared.tile([P, T], I32, name="kw_pool", align_bytes=64, offset=0)
         nc.sync.dma_start(kw_pool[:], k_words[0].rearrange("g t b -> g (t b)").bitcast(I32))
 
@@ -75,7 +76,7 @@ def tile_attend_pkv4_silu_kernel(tc, qT, k_words, k_scales, v_words, v_scales, v
         for o in range(PASSES):
             nc.scalar.copy(q_bf[:, o], q_raw[:, o].rearrange("p (j q) -> p q j", j=PACK))
 
-        ks_words = keep.tile([P, PASSES * N // 4], I32, name="ks_words", align_bytes=64)
+        ks_words = keep.tile([P, PASSES * N // 4], I32, name="ks_words", tag="planes", align_bytes=64)
         nc.gpsimd.memset(ks_words[:], 0)
         ks_plane = [ks_words[:].bitcast(U8)[:, o * N : (o + 1) * N] for o in range(PASSES)]
         ks_got = keep.tile([P, N], U8, name="ks_got", tag="scales_then_values", align_bytes=64)
@@ -104,7 +105,7 @@ def tile_attend_pkv4_silu_kernel(tc, qT, k_words, k_scales, v_words, v_scales, v
         vsc_got = keep.tile([P, PAGES * DV], U8, name="vsc_got", align_bytes=64)
         nc.vector.tensor_copy(vsc_got[:], vsc_pool[:].bitcast(U8).indirect(voffs_sb[:]))
 
-        q_codes = shared.tile([P, PASSES, NQ], U32, name="q_codes", align_bytes=64, offset=VS_AT)
+        q_codes = keep.tile([P, PASSES, NQ], U32, name="q_codes", align_bytes=64)
         q_scales = keep.tile([P, PASSES, NQ], U8, name="q_scales", align_bytes=64)
         nc.vector.quantize_mx(
             out=q_codes[:].rearrange("p o q -> p (o q)").bitcast(FP8X4),

@@ -24,8 +24,8 @@ PAGES = N // PAGE
 POOL_PAGES = T // PAGE
 QBLOCKS = NQ // P
 LIST_COLS = PAGE // 16
-VS_ROW = 8
-KS_ROW = 96
+VS_ROW = P - 1
+KS_ROW = 32
 VS_AT = 4 * T + 2 * PASSES * NQ * PACK
 GOT_AT = VS_AT + 4 * T
 SCORE_BANKS = 4
@@ -40,11 +40,13 @@ def tile_attend_pkv4_silu_kernel(tc, qT, k_words, k_scales, v_words, v_scales, v
 
         offs_sb = keep.tile([P, N // 16], U16, name="offs_sb")
         nc.sync.dma_start(offs_sb[:], offs)
+        ks_pool = keep.tile([P, T // 4], I32, name="ks_pool", tag="planes", align_bytes=64)
+        for o in range(PASSES):
+            nc.sync.dma_start(ks_pool[KS_ROW + o : KS_ROW + 32 : PASSES, :], k_scales.bitcast(I32)[o])
         voffs_sb = keep.tile([P, PAGES * DV // 16], U16, name="voffs_sb")
         nc.sync.dma_start(voffs_sb[:], voffs)
-        ks_pool = keep.tile([P, T // 4], I32, name="ks_pool", align_bytes=64)
-        for o in range(PASSES):
-            nc.sync.dma_start(ks_pool[KS_ROW + o : P : PASSES, :], k_scales.bitcast(I32)[o])
+        vs_pool = shared.tile([P, T], F32, name="vs_pool", align_bytes=64, offset=VS_AT)
+        nc.sync.dma_start(vs_pool[VS_ROW : VS_ROW + 1, :], vs[0:1, :])
         q_raw = keep.tile([P, PASSES, PACK * NQ], F32, name="q_raw", align_bytes=64)
         q_rows = qT[0].rearrange("(o p j) q -> o p (j q)", o=PASSES, j=PACK)
         for o in range(PASSES):
@@ -59,25 +61,22 @@ def tile_attend_pkv4_silu_kernel(tc, qT, k_words, k_scales, v_words, v_scales, v
                 vsc_rows[4 * c : 4 * c + 4],
             )
 
-        vs_pool = shared.tile([P, T], F32, name="vs_pool", align_bytes=64, offset=VS_AT)
-        nc.vector.memset(vs_pool[:].bitcast(I32), 0)
-        nc.sync.dma_start(vs_pool[VS_ROW : VS_ROW + 1, :], vs[0:1, :])
+        nc.vector.memset(ks_pool[0:KS_ROW, :], 0)
+        nc.vector.memset(ks_pool[KS_ROW + 32 : P, :], 0)
+        nc.vector.memset(vs_pool[0:VS_ROW, :].bitcast(I32), 0)
 
-        warm = shared.tile([P, 32], F32, name="warm", align_bytes=64, offset=4 * T - 64)
-        nc.vector.memset(warm[:, 0:1], 0.0)
-        warmed = keep.tile([P, 1], F32, name="warmed", tag="planes", align_bytes=64)
-        nc.scalar.activation(warmed[:], warm[:, 0:1], ACT.Silu)
+        warm = keep.tile([P, 1], F32, name="warm")
+        nc.gpsimd.memset(warm[:], 0.0)
+        warmed = keep.tile([P, 1], F32, name="warmed")
+        nc.scalar.activation(warmed[:], warm[:], ACT.Silu)
         kw_pool = shared.tile([P, T], I32, name="kw_pool", align_bytes=64, offset=0)
         nc.sync.dma_start(kw_pool[:], k_words[0].rearrange("g t b -> g (t b)").bitcast(I32))
-
-        nc.vector.memset(ks_pool[0:KS_ROW, :], 0)
 
         q_bf = shared.tile([P, PASSES, NQ, PACK], BF16, name="q_bf", align_bytes=64, offset=4 * T)
         for o in range(PASSES):
             nc.scalar.copy(q_bf[:, o], q_raw[:, o].rearrange("p (j q) -> p q j", j=PACK))
 
         ks_words = keep.tile([P, PASSES * N // 4], I32, name="ks_words", tag="planes", align_bytes=64)
-        nc.gpsimd.memset(ks_words[:], 0)
         ks_plane = [ks_words[:].bitcast(U8)[:, o * N : (o + 1) * N] for o in range(PASSES)]
         ks_got = keep.tile([P, N], U8, name="ks_got", tag="scales_then_values", align_bytes=64)
         nc.vector.tensor_copy(ks_got[:], ks_pool[:].bitcast(U8).indirect(offs_sb[:]))
@@ -86,7 +85,7 @@ def tile_attend_pkv4_silu_kernel(tc, qT, k_words, k_scales, v_words, v_scales, v
             ks_dealt[:].bitcast(U8).rearrange("p (g h t s) -> p h g t s", g=PAGES, h=2, t=PACK // 2),
             ks_got[:].rearrange("p (g s h t) -> p h g t s", g=PAGES, h=2, t=PACK // 2),
         )
-        for c in range(4):
+        for c in (0, 2, 1, 3):
             nc.sync.dma_start(ks_words[32 * c : 32 * c + 4, :], ks_dealt[KS_ROW + 8 * c : KS_ROW + 8 * c + 8, :])
         vw_pool = keep.tile([P, POOL_PAGES * DV], I32, name="vw_pool", tag="scales_then_values", align_bytes=64)
         nc.sync.dma_start(

@@ -29,6 +29,8 @@ KS_ROW = 32
 VS_AT = 4 * T + 2 * PASSES * NQ * PACK
 GOT_AT = VS_AT + 4 * T
 SCORE_BANKS = 4
+WARM_PASSES = 3
+ON_SCALAR = (0, 1)
 
 
 def tile_attend_pkv4_silu_kernel(tc, qT, k_words, k_scales, v_words, v_scales, vs, offs, voffs, out):
@@ -78,7 +80,7 @@ def tile_attend_pkv4_silu_kernel(tc, qT, k_words, k_scales, v_words, v_scales, v
 
         ks_words = keep.tile([P, PASSES * N // 4], I32, name="ks_words", tag="planes", align_bytes=64)
         ks_plane = [ks_words[:].bitcast(U8)[:, o * N : (o + 1) * N] for o in range(PASSES)]
-        ks_got = keep.tile([P, N], U8, name="ks_got", tag="scales_then_values", align_bytes=64)
+        ks_got = keep.tile([P, N], U8, name="ks_got", align_bytes=64)
         nc.vector.tensor_copy(ks_got[:], ks_pool[:].bitcast(U8).indirect(offs_sb[:]))
         ks_dealt = keep.tile([P, N // 4], I32, name="ks_dealt", align_bytes=64)
         nc.vector.tensor_copy(
@@ -87,11 +89,6 @@ def tile_attend_pkv4_silu_kernel(tc, qT, k_words, k_scales, v_words, v_scales, v
         )
         for c in (0, 2, 1, 3):
             nc.sync.dma_start(ks_words[32 * c : 32 * c + 4, :], ks_dealt[KS_ROW + 8 * c : KS_ROW + 8 * c + 8, :])
-        vw_pool = keep.tile([P, POOL_PAGES * DV], I32, name="vw_pool", tag="scales_then_values", align_bytes=64)
-        nc.sync.dma_start(
-            vw_pool[:].rearrange("g (u e) -> g u e", u=POOL_PAGES),
-            v_words.rearrange("u g e r -> g u (e r)").bitcast(I32),
-        )
 
         vs_got = keep.tile([P, N], F32, name="vs_got", align_bytes=64)
         nc.vector.tensor_copy(vs_got[:], vs_pool[:].indirect(offs_sb[:]))
@@ -100,6 +97,11 @@ def tile_attend_pkv4_silu_kernel(tc, qT, k_words, k_scales, v_words, v_scales, v
             col = keep.tile([P, PACK], F32, name=f"vs_col{g}")
             nc.sync.dma_start(col[:], vs_got[VS_ROW : VS_ROW + 1, g * PAGE : (g + 1) * PAGE])
             vs_col.append(col)
+        vw_pool = shared.tile([P, POOL_PAGES * DV], I32, name="vw_pool", align_bytes=64, offset=VS_AT)
+        nc.sync.dma_start(
+            vw_pool[:].rearrange("g (u e) -> g u e", u=POOL_PAGES),
+            v_words.rearrange("u g e r -> g u (e r)").bitcast(I32),
+        )
 
         vsc_got = keep.tile([P, PAGES * DV], U8, name="vsc_got", align_bytes=64)
         nc.vector.tensor_copy(vsc_got[:], vsc_pool[:].bitcast(U8).indirect(voffs_sb[:]))
@@ -112,33 +114,66 @@ def tile_attend_pkv4_silu_kernel(tc, qT, k_words, k_scales, v_words, v_scales, v
             in_=q_bf[:].rearrange("p o q j -> p (o q j)"),
         )
 
-        weights = []
-        for g in range(PAGES):
-            kw_got = shared.tile([P, PAGE], U32, name=f"kw_got{g}", align_bytes=64, offset=GOT_AT + 4 * PAGE * (g % 2))
+        def gather_keys(g):
+            kw_got = keep.tile([P, PAGE], U32, name=f"kw_got{g}", align_bytes=64)
             nc.vector.tensor_copy(kw_got[:], kw_pool[:].bitcast(U32).indirect(offs_sb[:, g * LIST_COLS : (g + 1) * LIST_COLS]))
-            keys = keep.tile([P, PASSES, 2 * PAGE], U8, name=f"keys{g}", align_bytes=64)
+            return kw_got
+
+        def part_keys(g, kw_got):
+            keys = shared.tile([P, PASSES, 2 * PAGE], U8, name=f"keys{g}", align_bytes=64, offset=GOT_AT + 4 * PAGE * g)
             halves = kw_got[:].bitcast(U16).rearrange("p (c i t o) -> p o c t i", i=4, t=PACK, o=PASSES)
             for o in range(PASSES):
                 nc.vector.tensor_copy(keys[:, o, :].bitcast(U16).rearrange("p (t c i) -> p c t i", t=PACK, i=4), halves[:, o])
+            return keys
+
+        spare = psum.tile([P, PAGE], F32, name="spare", tag=f"score{SCORE_BANKS - 1}")
+        for rep in range(WARM_PASSES):
+            nc.tensor.matmul_mx(
+                out=spare[:],
+                lhsT=kw_pool[:].bitcast(U8)[:, 0 : 2 * P].bitcast(FP4X4),
+                lhsT_scale=vsc_got[:, 0:P],
+                rhs=q_codes[:].rearrange("p o q -> p (o q)").bitcast(FP8X4),
+                rhs_scale=q_scales[:].rearrange("p o q -> p (o q)"),
+                start=True,
+                stop=True,
+            )
+
+        keys = []
+        got = gather_keys(0)
+        for g in range(PAGES):
+            ahead = gather_keys(g + 1) if g + 1 < PAGES else None
+            keys.append(part_keys(g, got))
+            got = ahead
+
+        weights = []
+        for g in range(PAGES):
             for b in range(QBLOCKS):
                 score = psum.tile([P, PACK, P], F32, name=f"score{g}_{b}", tag=f"score{(g * QBLOCKS + b) % SCORE_BANKS}")
                 for t in range(PACK):
                     for o in range(PASSES):
                         nc.tensor.matmul_mx(
                             out=score[:, t, :],
-                            lhsT=keys[:, o, 2 * P * t : 2 * P * (t + 1)].bitcast(FP4X4),
+                            lhsT=keys[g][:, o, 2 * P * t : 2 * P * (t + 1)].bitcast(FP4X4),
                             lhsT_scale=ks_plane[o][:, g * PAGE + P * t : g * PAGE + P * (t + 1)],
                             rhs=q_codes[:, o, b * P : (b + 1) * P].bitcast(FP8X4),
                             rhs_scale=q_scales[:, o, b * P : (b + 1) * P],
                             start=(o == 0),
                             stop=(o == PASSES - 1),
                         )
-                silu = keep.tile([P, P, PACK], F32, name=f"silu{g}_{b}", align_bytes=64)
-                nc.scalar.activation(silu[:], score[:].rearrange("p t q -> p q t"), ACT.Silu)
+                if (g, b) == ON_SCALAR:
+                    silu = keep.tile([P, PACK, P], F32, name=f"silu{g}_{b}", align_bytes=64)
+                    nc.scalar.activation(silu[:], score[:], ACT.Silu)
+                    by_place = keep.tile([P, PACK, P], BF16, name="by_place", align_bytes=64)
+                    for t in range(PACK):
+                        nc.scalar.activation(by_place[:, t], silu[:, t], ACT.Copy, scale=vs_col[g][:, t : t + 1])
+                else:
+                    silu = keep.tile([P, P, PACK], F32, name=f"silu{g}_{b}", align_bytes=64)
+                    nc.scalar.activation(silu[:], score[:].rearrange("p t q -> p q t"), ACT.Silu)
                 weights.append((g, b, silu))
 
-        vw_got = shared.tile([P, PAGES * DV], U32, name="vw_got", align_bytes=64, offset=GOT_AT + 4 * PAGE)
-        nc.vector.tensor_copy(vw_got[:], vw_pool[:].bitcast(U32).indirect(voffs_sb[:]))
+        w_scalar = shared.tile([P, P, PACK], BF16, name="w_scalar", align_bytes=64, offset=GOT_AT + 4 * PAGE * (PAGES - 1))
+        nc.scalar.copy(w_scalar[:].rearrange("p (c i) t -> p c t i", i=4), by_place[:].rearrange("p t (c i) -> p c t i", i=4))
+        vw_got = shared.tile([P, PAGES * DV], U32, name="vw_got", align_bytes=64, offset=GOT_AT)
 
         y = [psum.tile([P, DV], F32, name=f"y{b}", tag=f"score{((PAGES - 1) * QBLOCKS + b) % SCORE_BANKS}") for b in range(QBLOCKS)]
 
@@ -146,6 +181,8 @@ def tile_attend_pkv4_silu_kernel(tc, qT, k_words, k_scales, v_words, v_scales, v
             w_bf = keep.tile([P, P, PACK], BF16, name=f"w_bf{g}_{b}", align_bytes=64)
             nc.vector.tensor_tensor(w_bf[:], silu[:], vs_col[g][:].unsqueeze(1).to_broadcast([P, P, PACK]), MULT)
             return w_bf
+
+        opened = set()
 
         def multiply(g, b, w_bf):
             w_codes = keep.tile([P, P], U32, name=f"w_codes{g}_{b}", align_bytes=64)
@@ -159,19 +196,24 @@ def tile_attend_pkv4_silu_kernel(tc, qT, k_words, k_scales, v_words, v_scales, v
                 lhsT_scale=w_scales[:],
                 rhs=vw_got[:, g * DV : (g + 1) * DV].bitcast(FP8X4),
                 rhs_scale=vsc_got[:, g * DV : (g + 1) * DV],
-                start=(g == 0),
+                start=(b not in opened),
                 stop=(g == PAGES - 1),
             )
+            opened.add(b)
             if g == PAGES - 1:
                 result = keep.tile([P, DV], F32, name=f"result{b}")
                 nc.scalar.activation(result[:], y[b][:], ACT.Copy, scale=1.0 / 16.0)
                 queue = nc.sync if b == 0 else nc.scalar
                 queue.dma_start(out[0, b * P : (b + 1) * P, :], result[:])
 
+        order = [w for w in weights if w[:2] != ON_SCALAR]
         pending = None
-        for g, b, silu in weights:
+        for g, b, silu in order:
             w_bf = scale(g, b, silu)
-            if pending is not None:
+            if pending is None:
+                nc.vector.tensor_copy(vw_got[:], vw_pool[:].bitcast(U32).indirect(voffs_sb[:]))
+            else:
                 multiply(*pending)
             pending = (g, b, w_bf)
+        multiply(*ON_SCALAR, w_scalar)
         multiply(*pending)

@@ -1,6 +1,7 @@
 from contextlib import ExitStack
 
 import concourse.mybir as mybir
+from concourse.masks import make_identity
 
 N, T, D, DV, NQ = 1536, 4096, 1024, 128, 256
 PAGE = 512
@@ -25,164 +26,156 @@ POOL_PAGES = T // PAGE
 QBLOCKS = NQ // P
 LIST_COLS = PAGE // 16
 VS_ROW = P - 1
-KS_ROW = 32
-VS_AT = 4 * T + 2 * PASSES * NQ * PACK
-GOT_AT = VS_AT + 4 * T
-SCORE_BANKS = 4
-WARM_PASSES = 3
-ON_SCALAR = (0, 1)
+KS_ROW = P - 32
+VSC_ROW = P - 16
 
 
 def tile_attend_pkv4_silu_kernel(tc, qT, k_words, k_scales, v_words, v_scales, vs, offs, voffs, out):
     nc = tc.nc
     with ExitStack() as ctx:
         keep = ctx.enter_context(tc.tile_pool(name="keep", bufs=1))
-        shared = ctx.enter_context(tc.tile_pool(name="shared", bufs=1))
         psum = ctx.enter_context(tc.psum_pool(name="psum", bufs=1))
 
         offs_sb = keep.tile([P, N // 16], U16, name="offs_sb")
         nc.sync.dma_start(offs_sb[:], offs)
-        ks_pool = keep.tile([P, T // 4], I32, name="ks_pool", tag="planes", align_bytes=64)
-        for o in range(PASSES):
-            nc.sync.dma_start(ks_pool[KS_ROW + o : KS_ROW + 32 : PASSES, :], k_scales.bitcast(I32)[o])
+        ks_pool = keep.tile([P, T // 4], I32, name="ks_pool", align_bytes=64)
+        nc.sync.dma_start(ks_pool[KS_ROW:P, :], k_scales.bitcast(I32).rearrange("o f t -> f o t"))
+        vs_pool = keep.tile([P, T], F32, name="vs_pool", tag="planes", align_bytes=64)
+        nc.sync.dma_start(vs_pool[VS_ROW:P, :], vs[0:1, :])
         voffs_sb = keep.tile([P, PAGES * DV // 16], U16, name="voffs_sb")
         nc.sync.dma_start(voffs_sb[:], voffs)
-        vs_pool = shared.tile([P, T], F32, name="vs_pool", align_bytes=64, offset=VS_AT)
-        nc.sync.dma_start(vs_pool[VS_ROW : VS_ROW + 1, :], vs[0:1, :])
-        q_raw = keep.tile([P, PASSES, PACK * NQ], F32, name="q_raw", align_bytes=64)
-        q_rows = qT[0].rearrange("(o p j) q -> o p (j q)", o=PASSES, j=PACK)
-        for o in range(PASSES):
-            nc.sync.dma_start(q_raw[:, o], q_rows[o])
-
         vsc_pool = keep.tile([P, POOL_PAGES * DV // 4], I32, name="vsc_pool", align_bytes=64)
-        nc.gpsimd.memset(vsc_pool[:], 0)
-        vsc_rows = v_scales.bitcast(I32).rearrange("u f e -> f u e")
-        for c in range(4):
-            nc.sync.dma_start(
-                vsc_pool[32 * c : 32 * c + 4, :].rearrange("f (u e) -> f u e", u=POOL_PAGES),
-                vsc_rows[4 * c : 4 * c + 4],
-            )
+        nc.sync.dma_start(
+            vsc_pool[VSC_ROW:P, :].rearrange("f (u e) -> f u e", u=POOL_PAGES),
+            v_scales.bitcast(I32).rearrange("u f e -> f u e"),
+        )
+        kw_pool = keep.tile([P, T], I32, name="kw_pool", align_bytes=64)
+        nc.sync.dma_start(kw_pool[:], k_words[0].rearrange("g t b -> g (t b)").bitcast(I32))
+        q_rows = qT[0].rearrange("(o p j) q -> o p (j q)", o=PASSES, j=PACK)
+        q_raw = []
+        for o in range(PASSES):
+            raw = keep.tile([P, PACK * NQ], F32, name=f"q_raw{o}", tag=f"q_raw{o}", align_bytes=64)
+            nc.sync.dma_start(raw[:], q_rows[o])
+            q_raw.append(raw)
+        vw_pool = keep.tile([P, POOL_PAGES * DV], I32, name="vw_pool", align_bytes=64)
+        nc.sync.dma_start(
+            vw_pool[:].rearrange("g (u e) -> g u e", u=POOL_PAGES),
+            v_words.rearrange("u g e r -> g u (e r)").bitcast(I32),
+        )
 
         nc.vector.memset(ks_pool[0:KS_ROW, :], 0)
-        nc.vector.memset(ks_pool[KS_ROW + 32 : P, :], 0)
+        nc.vector.memset(vsc_pool[0:VSC_ROW, :], 0)
         nc.vector.memset(vs_pool[0:VS_ROW, :].bitcast(I32), 0)
 
         warm = keep.tile([P, 1], F32, name="warm")
         nc.gpsimd.memset(warm[:], 0.0)
         warmed = keep.tile([P, 1], F32, name="warmed")
         nc.scalar.activation(warmed[:], warm[:], ACT.Silu)
-        kw_pool = shared.tile([P, T], I32, name="kw_pool", align_bytes=64, offset=0)
-        nc.sync.dma_start(kw_pool[:], k_words[0].rearrange("g t b -> g (t b)").bitcast(I32))
+        ident = keep.tile([P, P], F32, name="ident", align_bytes=64)
+        make_identity(nc, ident[:])
 
-        q_bf = shared.tile([P, PASSES, NQ, PACK], BF16, name="q_bf", align_bytes=64, offset=4 * T)
-        for o in range(PASSES):
-            nc.scalar.copy(q_bf[:, o], q_raw[:, o].rearrange("p (j q) -> p q j", j=PACK))
+        vs_bank = psum.tile([P, PAGE], F32, name="vs_bank")
+        vs_col = []
+        for g in range(PAGES):
+            vs_got = keep.tile([P, PAGE], F32, name=f"vs_got{g}", align_bytes=64)
+            nc.scalar.activation(vs_got[:], vs_pool[:].indirect(offs_sb[:, g * LIST_COLS : (g + 1) * LIST_COLS]), ACT.Copy)
+            first = 2 * PACK * (PAGES - 1 - g)
+            for t in reversed(range(PACK)):
+                nc.tensor.transpose(vs_bank[:, first + 2 * t : first + 2 * t + P], vs_got[:, t:PAGE:PACK], ident[:])
+            vs_col.append(vs_bank[:, first + VS_ROW : first + VS_ROW + 2 * PACK : 2])
 
-        ks_words = keep.tile([P, PASSES * N // 4], I32, name="ks_words", tag="planes", align_bytes=64)
-        ks_plane = [ks_words[:].bitcast(U8)[:, o * N : (o + 1) * N] for o in range(PASSES)]
-        ks_got = keep.tile([P, N], U8, name="ks_got", align_bytes=64)
+        ks_got = keep.tile([P, N], U8, name="ks_got", tag="q_bf0", align_bytes=64)
         nc.vector.tensor_copy(ks_got[:], ks_pool[:].bitcast(U8).indirect(offs_sb[:]))
+        vsc_got = keep.tile([P, PAGES * DV], U8, name="vsc_got", align_bytes=64)
+        nc.vector.tensor_copy(vsc_got[:], vsc_pool[:].bitcast(U8).indirect(voffs_sb[:]))
         ks_dealt = keep.tile([P, N // 4], I32, name="ks_dealt", align_bytes=64)
         nc.vector.tensor_copy(
             ks_dealt[:].bitcast(U8).rearrange("p (g h t s) -> p h g t s", g=PAGES, h=2, t=PACK // 2),
             ks_got[:].rearrange("p (g s h t) -> p h g t s", g=PAGES, h=2, t=PACK // 2),
         )
+        ks_words = keep.tile([P, PASSES * N // 4], I32, name="ks_words", tag="planes", align_bytes=64)
+        ks_plane = [ks_words[:].bitcast(U8)[:, o * N : (o + 1) * N] for o in range(PASSES)]
         for c in (0, 2, 1, 3):
-            nc.sync.dma_start(ks_words[32 * c : 32 * c + 4, :], ks_dealt[KS_ROW + 8 * c : KS_ROW + 8 * c + 8, :])
-
-        vs_got = keep.tile([P, N], F32, name="vs_got", align_bytes=64)
-        nc.vector.tensor_copy(vs_got[:], vs_pool[:].indirect(offs_sb[:]))
-        vs_col = []
-        for g in range(PAGES):
-            col = keep.tile([P, PACK], F32, name=f"vs_col{g}")
-            nc.sync.dma_start(col[:], vs_got[VS_ROW : VS_ROW + 1, g * PAGE : (g + 1) * PAGE])
-            vs_col.append(col)
-        vw_pool = shared.tile([P, POOL_PAGES * DV], I32, name="vw_pool", align_bytes=64, offset=VS_AT)
-        nc.sync.dma_start(
-            vw_pool[:].rearrange("g (u e) -> g u e", u=POOL_PAGES),
-            v_words.rearrange("u g e r -> g u (e r)").bitcast(I32),
-        )
-
-        vsc_got = keep.tile([P, PAGES * DV], U8, name="vsc_got", align_bytes=64)
-        nc.vector.tensor_copy(vsc_got[:], vsc_pool[:].bitcast(U8).indirect(voffs_sb[:]))
+            nc.scalar.dma_start(ks_words[32 * c : 32 * c + 4, :], ks_dealt[KS_ROW + 8 * c : KS_ROW + 8 * c + 8, :])
 
         q_codes = keep.tile([P, PASSES, NQ], U32, name="q_codes", align_bytes=64)
         q_scales = keep.tile([P, PASSES, NQ], U8, name="q_scales", align_bytes=64)
-        nc.vector.quantize_mx(
-            out=q_codes[:].rearrange("p o q -> p (o q)").bitcast(FP8X4),
-            scales=q_scales[:].rearrange("p o q -> p (o q)"),
-            in_=q_bf[:].rearrange("p o q j -> p (o q j)"),
-        )
 
-        def gather_keys(g):
-            kw_got = keep.tile([P, PAGE], U32, name=f"kw_got{g}", align_bytes=64)
+        def cast_queries(o):
+            q_bf = keep.tile([P, NQ, PACK], BF16, name=f"q_bf{o}", tag=f"q_bf{o}", align_bytes=64)
+            nc.scalar.copy(
+                q_bf[:].rearrange("p (c i) j -> p c j i", i=4), q_raw[o][:].rearrange("p (j c i) -> p c j i", j=PACK, i=4)
+            )
+            return q_bf
+
+        def quantise_queries(o, q_bf):
+            nc.vector.quantize_mx(
+                out=q_codes[:, o].bitcast(FP8X4), scales=q_scales[:, o], in_=q_bf[:].rearrange("p q j -> p (q j)")
+            )
+
+        def gather_keys(g, tag):
+            kw_got = keep.tile([P, PAGE], U32, name=f"kw_got{g}", tag=tag, align_bytes=64)
             nc.vector.tensor_copy(kw_got[:], kw_pool[:].bitcast(U32).indirect(offs_sb[:, g * LIST_COLS : (g + 1) * LIST_COLS]))
             return kw_got
 
-        def part_keys(g, kw_got):
-            keys = shared.tile([P, PASSES, 2 * PAGE], U8, name=f"keys{g}", align_bytes=64, offset=GOT_AT + 4 * PAGE * g)
+        def part_keys(g, kw_got, tag):
+            keys = keep.tile([P, PASSES, 2 * PAGE], U8, name=f"keys{g}", tag=tag, align_bytes=64)
             halves = kw_got[:].bitcast(U16).rearrange("p (c i t o) -> p o c t i", i=4, t=PACK, o=PASSES)
             for o in range(PASSES):
                 nc.vector.tensor_copy(keys[:, o, :].bitcast(U16).rearrange("p (t c i) -> p c t i", t=PACK, i=4), halves[:, o])
             return keys
 
-        spare = psum.tile([P, PAGE], F32, name="spare", tag=f"score{SCORE_BANKS - 1}")
-        for rep in range(WARM_PASSES):
-            nc.tensor.matmul_mx(
-                out=spare[:],
-                lhsT=kw_pool[:].bitcast(U8)[:, 0 : 2 * P].bitcast(FP4X4),
-                lhsT_scale=vsc_got[:, 0:P],
-                rhs=q_codes[:].rearrange("p o q -> p (o q)").bitcast(FP8X4),
-                rhs_scale=q_scales[:].rearrange("p o q -> p (o q)"),
-                start=True,
-                stop=True,
-            )
+        q_bf = [cast_queries(o) for o in range(PASSES)]
+        got0 = gather_keys(0, "got0")
+        got1 = gather_keys(1, "got1")
+        keys = [part_keys(0, got0, "keys0")]
+        quantise_queries(0, q_bf[0])
+        keys.append(part_keys(1, got1, "q_raw0"))
+        got2 = gather_keys(2, "q_bf0")
+        quantise_queries(1, q_bf[1])
+        keys.append(part_keys(2, got2, "q_raw1"))
+        vw_got = keep.tile([P, PAGES * DV], U32, name="vw_got", tag="q_bf1", align_bytes=64)
+        nc.vector.tensor_copy(vw_got[:], vw_pool[:].bitcast(U32).indirect(voffs_sb[:]))
 
-        keys = []
-        got = gather_keys(0)
-        for g in range(PAGES):
-            ahead = gather_keys(g + 1) if g + 1 < PAGES else None
-            keys.append(part_keys(g, got))
-            got = ahead
+        vsc_words = keep.tile([P, PAGES * DV // 4], I32, name="vsc_words", tag="got0", align_bytes=64)
+        vsc_plane = vsc_words[:].bitcast(U8)
+        for c in range(4):
+            nc.sync.dma_start(vsc_words[32 * c : 32 * c + 4, :], vsc_got[:].bitcast(I32)[VSC_ROW + 4 * c : VSC_ROW + 4 * c + 4, :])
 
-        weights = []
-        for g in range(PAGES):
-            for b in range(QBLOCKS):
-                score = psum.tile([P, PACK, P], F32, name=f"score{g}_{b}", tag=f"score{(g * QBLOCKS + b) % SCORE_BANKS}")
-                for t in range(PACK):
-                    for o in range(PASSES):
-                        nc.tensor.matmul_mx(
-                            out=score[:, t, :],
-                            lhsT=keys[g][:, o, 2 * P * t : 2 * P * (t + 1)].bitcast(FP4X4),
-                            lhsT_scale=ks_plane[o][:, g * PAGE + P * t : g * PAGE + P * (t + 1)],
-                            rhs=q_codes[:, o, b * P : (b + 1) * P].bitcast(FP8X4),
-                            rhs_scale=q_scales[:, o, b * P : (b + 1) * P],
-                            start=(o == 0),
-                            stop=(o == PASSES - 1),
-                        )
-                if (g, b) == ON_SCALAR:
-                    silu = keep.tile([P, PACK, P], F32, name=f"silu{g}_{b}", align_bytes=64)
-                    nc.scalar.activation(silu[:], score[:], ACT.Silu)
-                    by_place = keep.tile([P, PACK, P], BF16, name="by_place", align_bytes=64)
-                    for t in range(PACK):
-                        nc.scalar.activation(by_place[:, t], silu[:, t], ACT.Copy, scale=vs_col[g][:, t : t + 1])
-                else:
-                    silu = keep.tile([P, P, PACK], F32, name=f"silu{g}_{b}", align_bytes=64)
-                    nc.scalar.activation(silu[:], score[:].rearrange("p t q -> p q t"), ACT.Silu)
-                weights.append((g, b, silu))
+        chunks = [(g, b) for g in range(PAGES) for b in range(QBLOCKS)]
+        score = {}
+        for g, b in chunks:
+            score[g, b] = psum.tile([P, PACK, P], F32, name=f"score{g}_{b}", tag=f"score{g}_{b}")
 
-        w_scalar = shared.tile([P, P, PACK], BF16, name="w_scalar", align_bytes=64, offset=GOT_AT + 4 * PAGE * (PAGES - 1))
-        nc.scalar.copy(w_scalar[:].rearrange("p (c i) t -> p c t i", i=4), by_place[:].rearrange("p t (c i) -> p c t i", i=4))
-        vw_got = shared.tile([P, PAGES * DV], U32, name="vw_got", align_bytes=64, offset=GOT_AT)
+        def score_pass(g, b, o):
+            for t in range(PACK):
+                nc.tensor.matmul_mx(
+                    out=score[g, b][:, t, :],
+                    lhsT=keys[g][:, o, 2 * P * t : 2 * P * (t + 1)].bitcast(FP4X4),
+                    lhsT_scale=ks_plane[o][:, g * PAGE + P * t : g * PAGE + P * (t + 1)],
+                    rhs=q_codes[:, o, b * P : (b + 1) * P].bitcast(FP8X4),
+                    rhs_scale=q_scales[:, o, b * P : (b + 1) * P],
+                    start=(o == 0 and t == 0),
+                    stop=(o == PASSES - 1 and t == PACK - 1),
+                )
 
-        y = [psum.tile([P, DV], F32, name=f"y{b}", tag=f"score{((PAGES - 1) * QBLOCKS + b) % SCORE_BANKS}") for b in range(QBLOCKS)]
+        early = chunks[: 2 * QBLOCKS]
+        for g, b in early:
+            score_pass(g, b, 0)
+        silu = {}
+        for g, b in chunks:
+            if (g, b) not in early:
+                score_pass(g, b, 0)
+            score_pass(g, b, 1)
+            silu[g, b] = keep.tile([P, P, PACK], F32, name=f"silu{g}_{b}", align_bytes=64)
+            nc.scalar.activation(silu[g, b][:], score[g, b][:].rearrange("p t q -> p q t"), ACT.Silu)
 
-        def scale(g, b, silu):
+        y = [psum.tile([P, DV], F32, name=f"y{b}", tag=f"score{PAGES - 1}_{b}") for b in range(QBLOCKS)]
+
+        def scale(g, b):
             w_bf = keep.tile([P, P, PACK], BF16, name=f"w_bf{g}_{b}", align_bytes=64)
-            nc.vector.tensor_tensor(w_bf[:], silu[:], vs_col[g][:].unsqueeze(1).to_broadcast([P, P, PACK]), MULT)
+            nc.vector.tensor_tensor(w_bf[:], silu[g, b][:], vs_col[g].unsqueeze(1).to_broadcast([P, P, PACK]), MULT)
             return w_bf
-
-        opened = set()
 
         def multiply(g, b, w_bf):
             w_codes = keep.tile([P, P], U32, name=f"w_codes{g}_{b}", align_bytes=64)
@@ -195,25 +188,20 @@ def tile_attend_pkv4_silu_kernel(tc, qT, k_words, k_scales, v_words, v_scales, v
                 lhsT=w_codes[:].bitcast(FP8X4),
                 lhsT_scale=w_scales[:],
                 rhs=vw_got[:, g * DV : (g + 1) * DV].bitcast(FP8X4),
-                rhs_scale=vsc_got[:, g * DV : (g + 1) * DV],
-                start=(b not in opened),
+                rhs_scale=vsc_plane[:, g * DV : (g + 1) * DV],
+                start=(g == 0),
                 stop=(g == PAGES - 1),
             )
-            opened.add(b)
             if g == PAGES - 1:
                 result = keep.tile([P, DV], F32, name=f"result{b}")
                 nc.scalar.activation(result[:], y[b][:], ACT.Copy, scale=1.0 / 16.0)
                 queue = nc.sync if b == 0 else nc.scalar
                 queue.dma_start(out[0, b * P : (b + 1) * P, :], result[:])
 
-        order = [w for w in weights if w[:2] != ON_SCALAR]
         pending = None
-        for g, b, silu in order:
-            w_bf = scale(g, b, silu)
-            if pending is None:
-                nc.vector.tensor_copy(vw_got[:], vw_pool[:].bitcast(U32).indirect(voffs_sb[:]))
-            else:
+        for g, b in chunks:
+            w_bf = scale(g, b)
+            if pending is not None:
                 multiply(*pending)
             pending = (g, b, w_bf)
-        multiply(*ON_SCALAR, w_scalar)
         multiply(*pending)

@@ -28,19 +28,21 @@ LIST_COLS = PAGE // 16
 VS_ROW = P - 1
 KS_ROW = P - 32
 VSC_ROW = P - 16
+ROW_BYTES = 4 * PACK * NQ
 
 
 def tile_attend_pkv4_silu_kernel(tc, qT, k_words, k_scales, v_words, v_scales, vs, offs, voffs, out):
     nc = tc.nc
     with ExitStack() as ctx:
         keep = ctx.enter_context(tc.tile_pool(name="keep", bufs=1))
+        shared = ctx.enter_context(tc.tile_pool(name="shared", bufs=1))
         psum = ctx.enter_context(tc.psum_pool(name="psum", bufs=1))
 
         offs_sb = keep.tile([P, N // 16], U16, name="offs_sb")
         nc.sync.dma_start(offs_sb[:], offs)
-        ks_pool = keep.tile([P, T // 4], I32, name="ks_pool", align_bytes=64)
+        ks_pool = keep.tile([P, T // 4], I32, name="ks_pool", tag="planes", align_bytes=64)
         nc.sync.dma_start(ks_pool[KS_ROW:P, :], k_scales.bitcast(I32).rearrange("o f t -> f o t"))
-        vs_pool = keep.tile([P, T], F32, name="vs_pool", tag="planes", align_bytes=64)
+        vs_pool = keep.tile([P, T], F32, name="vs_pool", tag="vs", align_bytes=64)
         nc.sync.dma_start(vs_pool[VS_ROW:P, :], vs[0:1, :])
         voffs_sb = keep.tile([P, PAGES * DV // 16], U16, name="voffs_sb")
         nc.sync.dma_start(voffs_sb[:], voffs)
@@ -49,19 +51,11 @@ def tile_attend_pkv4_silu_kernel(tc, qT, k_words, k_scales, v_words, v_scales, v
             vsc_pool[VSC_ROW:P, :].rearrange("f (u e) -> f u e", u=POOL_PAGES),
             v_scales.bitcast(I32).rearrange("u f e -> f u e"),
         )
+        q_rows = qT[0].rearrange("(o p j) q -> o p (j q)", o=PASSES, j=PACK)
+        q_raw0 = keep.tile([P, PACK * NQ], F32, name="q_raw0", align_bytes=64)
+        nc.sync.dma_start(q_raw0[:], q_rows[0])
         kw_pool = keep.tile([P, T], I32, name="kw_pool", align_bytes=64)
         nc.sync.dma_start(kw_pool[:], k_words[0].rearrange("g t b -> g (t b)").bitcast(I32))
-        q_rows = qT[0].rearrange("(o p j) q -> o p (j q)", o=PASSES, j=PACK)
-        q_raw = []
-        for o in range(PASSES):
-            raw = keep.tile([P, PACK * NQ], F32, name=f"q_raw{o}", tag=f"q_raw{o}", align_bytes=64)
-            nc.sync.dma_start(raw[:], q_rows[o])
-            q_raw.append(raw)
-        vw_pool = keep.tile([P, POOL_PAGES * DV], I32, name="vw_pool", align_bytes=64)
-        nc.sync.dma_start(
-            vw_pool[:].rearrange("g (u e) -> g u e", u=POOL_PAGES),
-            v_words.rearrange("u g e r -> g u (e r)").bitcast(I32),
-        )
 
         nc.vector.memset(ks_pool[0:KS_ROW, :], 0)
         nc.vector.memset(vsc_pool[0:VSC_ROW, :], 0)
@@ -84,7 +78,7 @@ def tile_attend_pkv4_silu_kernel(tc, qT, k_words, k_scales, v_words, v_scales, v
                 nc.tensor.transpose(vs_bank[:, first + 2 * t : first + 2 * t + P], vs_got[:, t:PAGE:PACK], ident[:])
             vs_col.append(vs_bank[:, first + VS_ROW : first + VS_ROW + 2 * PACK : 2])
 
-        ks_got = keep.tile([P, N], U8, name="ks_got", tag="q_bf0", align_bytes=64)
+        ks_got = shared.tile([P, N], U8, name="ks_got", align_bytes=64, offset=ROW_BYTES - N // 2)
         nc.vector.tensor_copy(ks_got[:], ks_pool[:].bitcast(U8).indirect(offs_sb[:]))
         vsc_got = keep.tile([P, PAGES * DV], U8, name="vsc_got", align_bytes=64)
         nc.vector.tensor_copy(vsc_got[:], vsc_pool[:].bitcast(U8).indirect(voffs_sb[:]))
@@ -96,13 +90,21 @@ def tile_attend_pkv4_silu_kernel(tc, qT, k_words, k_scales, v_words, v_scales, v
         ks_words = keep.tile([P, PASSES * N // 4], I32, name="ks_words", tag="planes", align_bytes=64)
         ks_plane = [ks_words[:].bitcast(U8)[:, o * N : (o + 1) * N] for o in range(PASSES)]
         for c in (0, 2, 1, 3):
-            nc.scalar.dma_start(ks_words[32 * c : 32 * c + 4, :], ks_dealt[KS_ROW + 8 * c : KS_ROW + 8 * c + 8, :])
+            nc.sync.dma_start(ks_words[32 * c : 32 * c + 4, :], ks_dealt[KS_ROW + 8 * c : KS_ROW + 8 * c + 8, :])
+        q_raw1 = shared.tile([P, PACK * NQ], F32, name="q_raw1", align_bytes=64, offset=0)
+        nc.sync.dma_start(q_raw1[:], q_rows[1])
+        q_raw = [q_raw0, q_raw1]
+        vw_pool = shared.tile([P, POOL_PAGES * DV], I32, name="vw_pool", align_bytes=64, offset=ROW_BYTES)
+        nc.sync.dma_start(
+            vw_pool[:].rearrange("g (u e) -> g u e", u=POOL_PAGES),
+            v_words.rearrange("u g e r -> g u (e r)").bitcast(I32),
+        )
 
         q_codes = keep.tile([P, PASSES, NQ], U32, name="q_codes", align_bytes=64)
         q_scales = keep.tile([P, PASSES, NQ], U8, name="q_scales", align_bytes=64)
 
-        def cast_queries(o):
-            q_bf = keep.tile([P, NQ, PACK], BF16, name=f"q_bf{o}", tag=f"q_bf{o}", align_bytes=64)
+        def cast_queries(o, tag):
+            q_bf = keep.tile([P, NQ, PACK], BF16, name=f"q_bf{o}", tag=tag, align_bytes=64)
             nc.scalar.copy(
                 q_bf[:].rearrange("p (c i) j -> p c j i", i=4), q_raw[o][:].rearrange("p (j c i) -> p c j i", j=PACK, i=4)
             )
@@ -113,27 +115,33 @@ def tile_attend_pkv4_silu_kernel(tc, qT, k_words, k_scales, v_words, v_scales, v
                 out=q_codes[:, o].bitcast(FP8X4), scales=q_scales[:, o], in_=q_bf[:].rearrange("p q j -> p (q j)")
             )
 
-        def gather_keys(g, tag):
-            kw_got = keep.tile([P, PAGE], U32, name=f"kw_got{g}", tag=tag, align_bytes=64)
+        def gather_keys(g):
+            kw_got = keep.tile([P, PAGE], U32, name=f"kw_got{g}", tag=f"got{g}", align_bytes=64)
             nc.vector.tensor_copy(kw_got[:], kw_pool[:].bitcast(U32).indirect(offs_sb[:, g * LIST_COLS : (g + 1) * LIST_COLS]))
             return kw_got
 
-        def part_keys(g, kw_got, tag):
-            keys = keep.tile([P, PASSES, 2 * PAGE], U8, name=f"keys{g}", tag=tag, align_bytes=64)
-            halves = kw_got[:].bitcast(U16).rearrange("p (c i t o) -> p o c t i", i=4, t=PACK, o=PASSES)
-            for o in range(PASSES):
-                nc.vector.tensor_copy(keys[:, o, :].bitcast(U16).rearrange("p (t c i) -> p c t i", t=PACK, i=4), halves[:, o])
-            return keys
+        keys = {}
 
-        q_bf = [cast_queries(o) for o in range(PASSES)]
-        got0 = gather_keys(0, "got0")
-        got1 = gather_keys(1, "got1")
-        keys = [part_keys(0, got0, "keys0")]
+        def part_keys(g, o, kw_got, tile):
+            halves = kw_got[:].bitcast(U16).rearrange("p (c i t o) -> p o c t i", i=4, t=PACK, o=PASSES)
+            nc.vector.tensor_copy(tile[:].bitcast(U16).rearrange("p (t c i) -> p c t i", t=PACK, i=4), halves[:, o])
+            keys[g, o] = tile
+
+        def key_tile(g, o):
+            return keep.tile([P, 2 * PAGE], U8, name=f"keys{g}_{o}", align_bytes=64)
+
+        q_bf = [cast_queries(0, "vs"), cast_queries(1, "q_bf1")]
         quantise_queries(0, q_bf[0])
-        keys.append(part_keys(1, got1, "q_raw0"))
-        got2 = gather_keys(2, "q_bf0")
+        got0 = gather_keys(0)
+        got1 = gather_keys(1)
+        part_keys(0, 0, got0, key_tile(0, 0))
+        part_keys(1, 0, got1, key_tile(1, 0))
+        got2 = gather_keys(2)
+        part_keys(0, 1, got0, key_tile(0, 1))
         quantise_queries(1, q_bf[1])
-        keys.append(part_keys(2, got2, "q_raw1"))
+        for g, o, at in ((2, 0, 0), (1, 1, 2 * PAGE), (2, 1, 4 * PAGE)):
+            tile = shared.tile([P, 2 * PAGE], U8, name=f"keys{g}_{o}", align_bytes=64, offset=at)
+            part_keys(g, o, (got0, got1, got2)[g], tile)
         vw_got = keep.tile([P, PAGES * DV], U32, name="vw_got", tag="q_bf1", align_bytes=64)
         nc.vector.tensor_copy(vw_got[:], vw_pool[:].bitcast(U32).indirect(voffs_sb[:]))
 
@@ -151,7 +159,7 @@ def tile_attend_pkv4_silu_kernel(tc, qT, k_words, k_scales, v_words, v_scales, v
             for t in range(PACK):
                 nc.tensor.matmul_mx(
                     out=score[g, b][:, t, :],
-                    lhsT=keys[g][:, o, 2 * P * t : 2 * P * (t + 1)].bitcast(FP4X4),
+                    lhsT=keys[g, o][:, 2 * P * t : 2 * P * (t + 1)].bitcast(FP4X4),
                     lhsT_scale=ks_plane[o][:, g * PAGE + P * t : g * PAGE + P * (t + 1)],
                     rhs=q_codes[:, o, b * P : (b + 1) * P].bitcast(FP8X4),
                     rhs_scale=q_scales[:, o, b * P : (b + 1) * P],
@@ -159,13 +167,13 @@ def tile_attend_pkv4_silu_kernel(tc, qT, k_words, k_scales, v_words, v_scales, v
                     stop=(o == PASSES - 1 and t == PACK - 1),
                 )
 
-        early = chunks[: 2 * QBLOCKS]
-        for g, b in early:
+        for g, b in chunks[: 2 * QBLOCKS]:
             score_pass(g, b, 0)
         silu = {}
         for g, b in chunks:
-            if (g, b) not in early:
-                score_pass(g, b, 0)
+            if (g, b) == (1, 0):
+                for late in range(QBLOCKS):
+                    score_pass(PAGES - 1, late, 0)
             score_pass(g, b, 1)
             silu[g, b] = keep.tile([P, P, PACK], F32, name=f"silu{g}_{b}", align_bytes=64)
             nc.scalar.activation(silu[g, b][:], score[g, b][:].rearrange("p t q -> p q t"), ACT.Silu)

@@ -1,7 +1,6 @@
 from contextlib import ExitStack
 
 import concourse.mybir as mybir
-from concourse.masks import make_identity
 
 N, T, D, DV, NQ = 1536, 4096, 1024, 128, 256
 PAGE = 512
@@ -42,7 +41,7 @@ def tile_attend_pkv4_silu_kernel(tc, qT, k_words, k_scales, v_words, v_scales, v
         nc.sync.dma_start(offs_sb[:], offs)
         ks_pool = keep.tile([P, T // 4], I32, name="ks_pool", tag="planes", align_bytes=64)
         nc.sync.dma_start(ks_pool[KS_ROW:P, :], k_scales.bitcast(I32).rearrange("o f t -> f o t"))
-        vs_pool = keep.tile([P, T], F32, name="vs_pool", tag="vs", align_bytes=64)
+        vs_pool = keep.tile([P, T], F32, name="vs_pool", align_bytes=64)
         nc.sync.dma_start(vs_pool[VS_ROW:P, :], vs[0:1, :])
         voffs_sb = keep.tile([P, PAGES * DV // 16], U16, name="voffs_sb")
         nc.sync.dma_start(voffs_sb[:], voffs)
@@ -52,10 +51,13 @@ def tile_attend_pkv4_silu_kernel(tc, qT, k_words, k_scales, v_words, v_scales, v
             v_scales.bitcast(I32).rearrange("u f e -> f u e"),
         )
         q_rows = qT[0].rearrange("(o p j) q -> o p (j q)", o=PASSES, j=PACK)
-        q_raw0 = keep.tile([P, PACK * NQ], F32, name="q_raw0", align_bytes=64)
+        q_raw0 = keep.tile([P, PACK * NQ], F32, name="q_raw0", tag="q_raw0", align_bytes=64)
         nc.sync.dma_start(q_raw0[:], q_rows[0])
         kw_pool = keep.tile([P, T], I32, name="kw_pool", align_bytes=64)
         nc.sync.dma_start(kw_pool[:], k_words[0].rearrange("g t b -> g (t b)").bitcast(I32))
+        q_raw1 = shared.tile([P, PACK * NQ], F32, name="q_raw1", align_bytes=64, offset=0)
+        nc.sync.dma_start(q_raw1[:], q_rows[1])
+        q_raw = [q_raw0, q_raw1]
 
         nc.vector.memset(ks_pool[0:KS_ROW, :], 0)
         nc.vector.memset(vsc_pool[0:VSC_ROW, :], 0)
@@ -65,20 +67,8 @@ def tile_attend_pkv4_silu_kernel(tc, qT, k_words, k_scales, v_words, v_scales, v
         nc.gpsimd.memset(warm[:], 0.0)
         warmed = keep.tile([P, 1], F32, name="warmed")
         nc.scalar.activation(warmed[:], warm[:], ACT.Silu)
-        ident = keep.tile([P, P], F32, name="ident", align_bytes=64)
-        make_identity(nc, ident[:])
 
-        vs_bank = psum.tile([P, PAGE], F32, name="vs_bank")
-        vs_col = []
-        for g in range(PAGES):
-            vs_got = keep.tile([P, PAGE], F32, name=f"vs_got{g}", align_bytes=64)
-            nc.scalar.activation(vs_got[:], vs_pool[:].indirect(offs_sb[:, g * LIST_COLS : (g + 1) * LIST_COLS]), ACT.Copy)
-            first = 2 * PACK * (PAGES - 1 - g)
-            for t in reversed(range(PACK)):
-                nc.tensor.transpose(vs_bank[:, first + 2 * t : first + 2 * t + P], vs_got[:, t:PAGE:PACK], ident[:])
-            vs_col.append(vs_bank[:, first + VS_ROW : first + VS_ROW + 2 * PACK : 2])
-
-        ks_got = shared.tile([P, N], U8, name="ks_got", align_bytes=64, offset=ROW_BYTES - N // 2)
+        ks_got = shared.tile([P, N], U8, name="ks_got", align_bytes=64, offset=ROW_BYTES)
         nc.vector.tensor_copy(ks_got[:], ks_pool[:].bitcast(U8).indirect(offs_sb[:]))
         vsc_got = keep.tile([P, PAGES * DV], U8, name="vsc_got", align_bytes=64)
         nc.vector.tensor_copy(vsc_got[:], vsc_pool[:].bitcast(U8).indirect(voffs_sb[:]))
@@ -91,10 +81,7 @@ def tile_attend_pkv4_silu_kernel(tc, qT, k_words, k_scales, v_words, v_scales, v
         ks_plane = [ks_words[:].bitcast(U8)[:, o * N : (o + 1) * N] for o in range(PASSES)]
         for c in (0, 2, 1, 3):
             nc.sync.dma_start(ks_words[32 * c : 32 * c + 4, :], ks_dealt[KS_ROW + 8 * c : KS_ROW + 8 * c + 8, :])
-        q_raw1 = shared.tile([P, PACK * NQ], F32, name="q_raw1", align_bytes=64, offset=0)
-        nc.sync.dma_start(q_raw1[:], q_rows[1])
-        q_raw = [q_raw0, q_raw1]
-        vw_pool = shared.tile([P, POOL_PAGES * DV], I32, name="vw_pool", align_bytes=64, offset=ROW_BYTES)
+        vw_pool = shared.tile([P, POOL_PAGES * DV], I32, name="vw_pool", align_bytes=64, offset=ROW_BYTES + 128)
         nc.sync.dma_start(
             vw_pool[:].rearrange("g (u e) -> g u e", u=POOL_PAGES),
             v_words.rearrange("u g e r -> g u (e r)").bitcast(I32),
@@ -130,18 +117,27 @@ def tile_attend_pkv4_silu_kernel(tc, qT, k_words, k_scales, v_words, v_scales, v
         def key_tile(g, o):
             return keep.tile([P, 2 * PAGE], U8, name=f"keys{g}_{o}", align_bytes=64)
 
-        q_bf = [cast_queries(0, "vs"), cast_queries(1, "q_bf1")]
+        q_bf = [cast_queries(0, "q_bf0")]
+        vs_got = keep.tile([P, N], F32, name="vs_got", tag="q_raw0", align_bytes=64)
+        nc.scalar.activation(vs_got[:], vs_pool[:].indirect(offs_sb[:]), ACT.Copy)
+        vs_col = []
+        for g in range(PAGES):
+            col = shared.tile([P, PACK], F32, name=f"vs_col{g}", offset=ROW_BYTES + 32 * g)
+            nc.sync.dma_start(col[:], vs_got[VS_ROW:P, g * PAGE : (g + 1) * PAGE])
+            vs_col.append(col[:])
+        q_bf.append(cast_queries(1, "q_bf1"))
         quantise_queries(0, q_bf[0])
         got0 = gather_keys(0)
         got1 = gather_keys(1)
         part_keys(0, 0, got0, key_tile(0, 0))
-        part_keys(1, 0, got1, key_tile(1, 0))
-        got2 = gather_keys(2)
         part_keys(0, 1, got0, key_tile(0, 1))
+        got2 = gather_keys(2)
         quantise_queries(1, q_bf[1])
-        for g, o, at in ((2, 0, 0), (1, 1, 2 * PAGE), (2, 1, 4 * PAGE)):
-            tile = shared.tile([P, 2 * PAGE], U8, name=f"keys{g}_{o}", align_bytes=64, offset=at)
-            part_keys(g, o, (got0, got1, got2)[g], tile)
+        for g, got in ((1, got1), (2, got2)):
+            for o in range(PASSES):
+                at = 2 * PAGE * (PASSES * (g - 1) + o)
+                tile = shared.tile([P, 2 * PAGE], U8, name=f"keys{g}_{o}", align_bytes=64, offset=at)
+                part_keys(g, o, got, tile)
         vw_got = keep.tile([P, PAGES * DV], U32, name="vw_got", tag="q_bf1", align_bytes=64)
         nc.vector.tensor_copy(vw_got[:], vw_pool[:].bitcast(U32).indirect(voffs_sb[:]))
 
@@ -167,13 +163,12 @@ def tile_attend_pkv4_silu_kernel(tc, qT, k_words, k_scales, v_words, v_scales, v
                     stop=(o == PASSES - 1 and t == PACK - 1),
                 )
 
-        for g, b in chunks[: 2 * QBLOCKS]:
+        for g, b in chunks[:QBLOCKS]:
             score_pass(g, b, 0)
         silu = {}
         for g, b in chunks:
-            if (g, b) == (1, 0):
-                for late in range(QBLOCKS):
-                    score_pass(PAGES - 1, late, 0)
+            if g > 0:
+                score_pass(g, b, 0)
             score_pass(g, b, 1)
             silu[g, b] = keep.tile([P, P, PACK], F32, name=f"silu{g}_{b}", align_bytes=64)
             nc.scalar.activation(silu[g, b][:], score[g, b][:].rearrange("p t q -> p q t"), ACT.Silu)

@@ -25,7 +25,7 @@ POOL_PAGES = T // PAGE
 QBLOCKS = NQ // P
 LIST_COLS = PAGE // 16
 VS_ROW = P - 1
-KS_ROW = P - 32
+KS_ROW = 32
 VSC_ROW = P - 16
 ROW_BYTES = 4 * PACK * NQ
 
@@ -40,7 +40,7 @@ def tile_attend_pkv4_silu_kernel(tc, qT, k_words, k_scales, v_words, v_scales, v
         offs_sb = keep.tile([P, N // 16], U16, name="offs_sb")
         nc.sync.dma_start(offs_sb[:], offs)
         ks_pool = keep.tile([P, T // 4], I32, name="ks_pool", tag="planes", align_bytes=64)
-        nc.sync.dma_start(ks_pool[KS_ROW:P, :], k_scales.bitcast(I32).rearrange("o f t -> f o t"))
+        nc.sync.dma_start(ks_pool[KS_ROW : KS_ROW + 32, :], k_scales.bitcast(I32).rearrange("o f t -> f o t"))
         vs_pool = keep.tile([P, T], F32, name="vs_pool", align_bytes=64)
         nc.sync.dma_start(vs_pool[VS_ROW:P, :], vs[0:1, :])
         voffs_sb = keep.tile([P, PAGES * DV // 16], U16, name="voffs_sb")
@@ -60,6 +60,7 @@ def tile_attend_pkv4_silu_kernel(tc, qT, k_words, k_scales, v_words, v_scales, v
         q_raw = [q_raw0, q_raw1]
 
         nc.vector.memset(ks_pool[0:KS_ROW, :], 0)
+        nc.vector.memset(ks_pool[KS_ROW + 32 : P, :], 0)
         nc.vector.memset(vsc_pool[0:VSC_ROW, :], 0)
         nc.vector.memset(vs_pool[0:VS_ROW, :].bitcast(I32), 0)
 

@@ -27,6 +27,7 @@ LIST_COLS = PAGE // 16
 VS_ROW = P - 1
 KS_ROW = 32
 VSC_ROW = P - 16
+ODD_SPLIT = T // 8 + 1
 ROW_BYTES = 4 * PACK * NQ
 
 
@@ -59,13 +60,14 @@ def tile_attend_pkv4_silu_kernel(tc, qT, k_words, k_scales, v_words, v_scales, v
         nc.sync.dma_start(q_raw1[:], q_rows[1])
         q_raw = [q_raw0, q_raw1]
 
-        nc.vector.memset(ks_pool[0:KS_ROW, :], 0)
-        nc.vector.memset(ks_pool[KS_ROW + 32 : P, :], 0)
-        nc.vector.memset(vsc_pool[0:VSC_ROW, :], 0)
-        nc.vector.memset(vs_pool[0:VS_ROW, :].bitcast(I32), 0)
+        for rows in (slice(0, KS_ROW), slice(KS_ROW + 32, P)):
+            for cols in (slice(0, ODD_SPLIT), slice(ODD_SPLIT, T // 4)):
+                nc.vector.memset(ks_pool[rows, cols], 0)
 
         warm = keep.tile([P, 1], F32, name="warm")
         nc.gpsimd.memset(warm[:], 0.0)
+        nc.gpsimd.memset(vsc_pool[0:VSC_ROW, :], 0)
+        nc.gpsimd.memset(vs_pool[0:VS_ROW, :].bitcast(I32), 0)
         warmed = keep.tile([P, 1], F32, name="warmed")
         nc.scalar.activation(warmed[:], warm[:], ACT.Silu)
 

@@ -29,6 +29,7 @@ KS_ROW = 32
 VSC_ROW = P - 16
 ODD_SPLIT = T // 8 + 1
 ROW_BYTES = 4 * PACK * NQ
+Q0_AT = 3 * ROW_BYTES
 
 
 def tile_attend_pkv4_silu_kernel(tc, qT, k_words, k_scales, v_words, v_scales, vs, offs, voffs, out):
@@ -52,10 +53,10 @@ def tile_attend_pkv4_silu_kernel(tc, qT, k_words, k_scales, v_words, v_scales, v
             v_scales.bitcast(I32).rearrange("u f e -> f u e"),
         )
         q_rows = qT[0].rearrange("(o p j) q -> o p (j q)", o=PASSES, j=PACK)
-        q_raw0 = keep.tile([P, PACK * NQ], F32, name="q_raw0", tag="q_raw0", align_bytes=64)
-        nc.sync.dma_start(q_raw0[:], q_rows[0])
         kw_pool = keep.tile([P, T], I32, name="kw_pool", align_bytes=64)
         nc.sync.dma_start(kw_pool[:], k_words[0].rearrange("g t b -> g (t b)").bitcast(I32))
+        q_raw0 = shared.tile([P, PACK * NQ], F32, name="q_raw0", align_bytes=64, offset=Q0_AT)
+        nc.sync.dma_start(q_raw0[:], q_rows[0])
         q_raw1 = shared.tile([P, PACK * NQ], F32, name="q_raw1", align_bytes=64, offset=0)
         nc.sync.dma_start(q_raw1[:], q_rows[1])
         q_raw = [q_raw0, q_raw1]
@@ -84,11 +85,6 @@ def tile_attend_pkv4_silu_kernel(tc, qT, k_words, k_scales, v_words, v_scales, v
         ks_plane = [ks_words[:].bitcast(U8)[:, o * N : (o + 1) * N] for o in range(PASSES)]
         for c in (0, 2, 1, 3):
             nc.sync.dma_start(ks_words[32 * c : 32 * c + 4, :], ks_dealt[KS_ROW + 8 * c : KS_ROW + 8 * c + 8, :])
-        vw_pool = shared.tile([P, POOL_PAGES * DV], I32, name="vw_pool", align_bytes=64, offset=ROW_BYTES + 128)
-        nc.sync.dma_start(
-            vw_pool[:].rearrange("g (u e) -> g u e", u=POOL_PAGES),
-            v_words.rearrange("u g e r -> g u (e r)").bitcast(I32),
-        )
 
         q_codes = keep.tile([P, PASSES, NQ], U32, name="q_codes", align_bytes=64)
         q_scales = keep.tile([P, PASSES, NQ], U8, name="q_scales", align_bytes=64)
@@ -106,7 +102,10 @@ def tile_attend_pkv4_silu_kernel(tc, qT, k_words, k_scales, v_words, v_scales, v
             )
 
         def gather_keys(g):
-            kw_got = keep.tile([P, PAGE], U32, name=f"kw_got{g}", tag=f"got{g}", align_bytes=64)
+            if g == PAGES - 1:
+                kw_got = shared.tile([P, PAGE], U32, name=f"kw_got{g}", align_bytes=64, offset=Q0_AT)
+            else:
+                kw_got = keep.tile([P, PAGE], U32, name=f"kw_got{g}", tag=f"got{g}", align_bytes=64)
             nc.vector.tensor_copy(kw_got[:], kw_pool[:].bitcast(U32).indirect(offs_sb[:, g * LIST_COLS : (g + 1) * LIST_COLS]))
             return kw_got
 
@@ -120,20 +119,30 @@ def tile_attend_pkv4_silu_kernel(tc, qT, k_words, k_scales, v_words, v_scales, v
         def key_tile(g, o):
             return keep.tile([P, 2 * PAGE], U8, name=f"keys{g}_{o}", align_bytes=64)
 
-        q_bf = [cast_queries(0, "q_bf0")]
-        vs_got = keep.tile([P, N], F32, name="vs_got", tag="q_raw0", align_bytes=64)
-        nc.scalar.activation(vs_got[:], vs_pool[:].indirect(offs_sb[:]), ACT.Copy)
-        vs_col = []
+        vs_got = []
         for g in range(PAGES):
+            got = keep.tile([P, PAGE], F32, name=f"vs_got{g}", align_bytes=64)
+            nc.scalar.activation(got[:], vs_pool[:].indirect(offs_sb[:, g * LIST_COLS : (g + 1) * LIST_COLS]), ACT.Copy)
+            vs_got.append(got)
+
+        def place_column(g):
             col = shared.tile([P, PACK], F32, name=f"vs_col{g}", offset=ROW_BYTES + 32 * g)
-            nc.sync.dma_start(col[:], vs_got[VS_ROW:P, g * PAGE : (g + 1) * PAGE])
-            vs_col.append(col[:])
-        q_bf.append(cast_queries(1, "q_bf1"))
-        quantise_queries(0, q_bf[0])
+            nc.sync.dma_start(col[:], vs_got[g][VS_ROW:P, :])
+            return col[:]
+
+        vs_col = [place_column(0)]
+        vw_pool = shared.tile([P, POOL_PAGES * DV], I32, name="vw_pool", align_bytes=64, offset=ROW_BYTES + 128)
+        nc.sync.dma_start(
+            vw_pool[:].rearrange("g (u e) -> g u e", u=POOL_PAGES),
+            v_words.rearrange("u g e r -> g u (e r)").bitcast(I32),
+        )
+        vs_col.extend(place_column(g) for g in range(1, PAGES))
+        q_bf = [cast_queries(o, f"q_bf{o}") for o in range(PASSES)]
         got0 = gather_keys(0)
         got1 = gather_keys(1)
         part_keys(0, 0, got0, key_tile(0, 0))
         part_keys(0, 1, got0, key_tile(0, 1))
+        quantise_queries(0, q_bf[0])
         got2 = gather_keys(2)
         quantise_queries(1, q_bf[1])
         for g, got in ((1, got1), (2, got2)):
@@ -179,7 +188,10 @@ def tile_attend_pkv4_silu_kernel(tc, qT, k_words, k_scales, v_words, v_scales, v
         y = [psum.tile([P, DV], F32, name=f"y{b}", tag=f"score{PAGES - 1}_{b}") for b in range(QBLOCKS)]
 
         def scale(g, b):
-            w_bf = keep.tile([P, P, PACK], BF16, name=f"w_bf{g}_{b}", align_bytes=64)
+            if (g, b) == (0, 0):
+                w_bf = shared.tile([P, P, PACK], BF16, name="w_bf0_0", align_bytes=64, offset=ROW_BYTES + 1024)
+            else:
+                w_bf = keep.tile([P, P, PACK], BF16, name=f"w_bf{g}_{b}", align_bytes=64)
             nc.vector.tensor_tensor(w_bf[:], silu[g, b][:], vs_col[g].unsqueeze(1).to_broadcast([P, P, PACK]), MULT)
             return w_bf
 

@@ -30,6 +30,7 @@ VSC_ROW = P - 16
 ODD_SPLIT = T // 8 + 1
 ROW_BYTES = 4 * PACK * NQ
 Q0_AT = 3 * ROW_BYTES
+KS_AT = 4 * ROW_BYTES
 
 
 def tile_attend_pkv4_silu_kernel(tc, qT, k_words, k_scales, v_words, v_scales, vs, offs, voffs, out):
@@ -41,7 +42,7 @@ def tile_attend_pkv4_silu_kernel(tc, qT, k_words, k_scales, v_words, v_scales, v
 
         offs_sb = keep.tile([P, N // 16], U16, name="offs_sb")
         nc.sync.dma_start(offs_sb[:], offs)
-        ks_pool = keep.tile([P, T // 4], I32, name="ks_pool", tag="planes", align_bytes=64)
+        ks_pool = shared.tile([P, T // 4], I32, name="ks_pool", align_bytes=64, offset=KS_AT)
         nc.sync.dma_start(ks_pool[KS_ROW : KS_ROW + 32, :], k_scales.bitcast(I32).rearrange("o f t -> f o t"))
         vs_pool = keep.tile([P, T], F32, name="vs_pool", align_bytes=64)
         nc.sync.dma_start(vs_pool[VS_ROW:P, :], vs[0:1, :])
@@ -81,24 +82,40 @@ def tile_attend_pkv4_silu_kernel(tc, qT, k_words, k_scales, v_words, v_scales, v
             ks_dealt[:].bitcast(U8).rearrange("p (g h t s) -> p h g t s", g=PAGES, h=2, t=PACK // 2),
             ks_got[:].rearrange("p (g s h t) -> p h g t s", g=PAGES, h=2, t=PACK // 2),
         )
-        ks_words = keep.tile([P, PASSES * N // 4], I32, name="ks_words", tag="planes", align_bytes=64)
-        ks_plane = [ks_words[:].bitcast(U8)[:, o * N : (o + 1) * N] for o in range(PASSES)]
-        for c in (0, 2, 1, 3):
-            nc.sync.dma_start(ks_words[32 * c : 32 * c + 4, :], ks_dealt[KS_ROW + 8 * c : KS_ROW + 8 * c + 8, :])
+        ks_plane = {}
 
-        q_codes = keep.tile([P, PASSES, NQ], U32, name="q_codes", align_bytes=64)
-        q_scales = keep.tile([P, PASSES, NQ], U8, name="q_scales", align_bytes=64)
+        def place_planes(first, count):
+            words = count * PAGE // 4
+            planes = shared.tile([P, PASSES * words], I32, name=f"planes{first}", align_bytes=64, offset=KS_AT + PASSES * PAGE * first)
+            for c in (0, 2, 1, 3):
+                rows = slice(KS_ROW + 8 * c, KS_ROW + 8 * c + 8)
+                nc.sync.dma_start(planes[32 * c : 32 * c + 4, :], ks_dealt[rows, first * PAGE // 4 : first * PAGE // 4 + words])
+            for g in range(count):
+                for o in range(PASSES):
+                    at = (o * count + g) * PAGE
+                    ks_plane[first + g, o] = planes[:].bitcast(U8)[:, at : at + PAGE]
 
-        def cast_queries(o, tag):
-            q_bf = keep.tile([P, NQ, PACK], BF16, name=f"q_bf{o}", tag=tag, align_bytes=64)
+        place_planes(0, 1)
+
+        q_codes = keep.tile([P, QBLOCKS * PASSES * P], U32, name="q_codes", align_bytes=64)
+        q_scales = keep.tile([P, QBLOCKS * PASSES * P], U8, name="q_scales", align_bytes=64)
+
+        q_bf = keep.tile([P, QBLOCKS * PASSES * P * PACK], BF16, name="q_bf", tag="q_bf", align_bytes=64)
+
+        def cast_queries(o, b):
+            at = (b * PASSES + o) * P * PACK
+            rows = q_raw[o][:].rearrange("p (j q) -> p j q", j=PACK)[:, :, b * P : (b + 1) * P]
             nc.scalar.copy(
-                q_bf[:].rearrange("p (c i) j -> p c j i", i=4), q_raw[o][:].rearrange("p (j c i) -> p c j i", j=PACK, i=4)
+                q_bf[:, at : at + P * PACK].rearrange("p (c i j) -> p c j i", i=4, j=PACK),
+                rows.rearrange("p j (c i) -> p c j i", i=4),
             )
-            return q_bf
 
-        def quantise_queries(o, q_bf):
+        def quantise_queries(first, count):
+            cols = slice(first * P, (first + count) * P)
             nc.vector.quantize_mx(
-                out=q_codes[:, o].bitcast(FP8X4), scales=q_scales[:, o], in_=q_bf[:].rearrange("p q j -> p (q j)")
+                out=q_codes[:, cols].bitcast(FP8X4),
+                scales=q_scales[:, cols],
+                in_=q_bf[:, first * P * PACK : (first + count) * P * PACK],
             )
 
         def gather_keys(g):
@@ -130,27 +147,29 @@ def tile_attend_pkv4_silu_kernel(tc, qT, k_words, k_scales, v_words, v_scales, v
             nc.sync.dma_start(col[:], vs_got[g][VS_ROW:P, :])
             return col[:]
 
-        vs_col = [place_column(0)]
         vw_pool = shared.tile([P, POOL_PAGES * DV], I32, name="vw_pool", align_bytes=64, offset=ROW_BYTES + 128)
         nc.sync.dma_start(
             vw_pool[:].rearrange("g (u e) -> g u e", u=POOL_PAGES),
             v_words.rearrange("u g e r -> g u (e r)").bitcast(I32),
         )
-        vs_col.extend(place_column(g) for g in range(1, PAGES))
-        q_bf = [cast_queries(o, f"q_bf{o}") for o in range(PASSES)]
+        place_planes(1, PAGES - 1)
+        vs_col = [place_column(g) for g in range(PAGES)]
+        for o in range(PASSES):
+            for b in range(QBLOCKS):
+                cast_queries(o, b)
         got0 = gather_keys(0)
         got1 = gather_keys(1)
         part_keys(0, 0, got0, key_tile(0, 0))
         part_keys(0, 1, got0, key_tile(0, 1))
-        quantise_queries(0, q_bf[0])
+        quantise_queries(0, 1)
         got2 = gather_keys(2)
-        quantise_queries(1, q_bf[1])
-        for g, got in ((1, got1), (2, got2)):
-            for o in range(PASSES):
-                at = 2 * PAGE * (PASSES * (g - 1) + o)
-                tile = shared.tile([P, 2 * PAGE], U8, name=f"keys{g}_{o}", align_bytes=64, offset=at)
-                part_keys(g, o, got, tile)
-        vw_got = keep.tile([P, PAGES * DV], U32, name="vw_got", tag="q_bf1", align_bytes=64)
+        quantise_queries(1, 1)
+        part_keys(1, 0, got1, shared.tile([P, 2 * PAGE], U8, name="keys1_0", align_bytes=64, offset=Q0_AT + 4 * PAGE))
+        quantise_queries(PASSES, PASSES)
+        for slot, (g, o, got) in enumerate(((1, 1, got1), (2, 0, got2), (2, 1, got2))):
+            tile = shared.tile([P, 2 * PAGE], U8, name=f"keys{g}_{o}", align_bytes=64, offset=2 * PAGE * slot)
+            part_keys(g, o, got, tile)
+        vw_got = keep.tile([P, PAGES * DV], U32, name="vw_got", tag="q_bf", align_bytes=64)
         nc.vector.tensor_copy(vw_got[:], vw_pool[:].bitcast(U32).indirect(voffs_sb[:]))
 
         vsc_words = keep.tile([P, PAGES * DV // 4], I32, name="vsc_words", tag="got0", align_bytes=64)
@@ -168,39 +187,36 @@ def tile_attend_pkv4_silu_kernel(tc, qT, k_words, k_scales, v_words, v_scales, v
                 nc.tensor.matmul_mx(
                     out=score[g, b][:, t, :],
                     lhsT=keys[g, o][:, 2 * P * t : 2 * P * (t + 1)].bitcast(FP4X4),
-                    lhsT_scale=ks_plane[o][:, g * PAGE + P * t : g * PAGE + P * (t + 1)],
-                    rhs=q_codes[:, o, b * P : (b + 1) * P].bitcast(FP8X4),
-                    rhs_scale=q_scales[:, o, b * P : (b + 1) * P],
+                    lhsT_scale=ks_plane[g, o][:, P * t : P * (t + 1)],
+                    rhs=q_codes[:, (b * PASSES + o) * P : (b * PASSES + o + 1) * P].bitcast(FP8X4),
+                    rhs_scale=q_scales[:, (b * PASSES + o) * P : (b * PASSES + o + 1) * P],
                     start=(o == 0 and t == 0),
                     stop=(o == PASSES - 1 and t == PACK - 1),
                 )
 
-        for g, b in chunks[:QBLOCKS]:
-            score_pass(g, b, 0)
         silu = {}
         for g, b in chunks:
-            if g > 0:
-                score_pass(g, b, 0)
-            score_pass(g, b, 1)
-            silu[g, b] = keep.tile([P, P, PACK], F32, name=f"silu{g}_{b}", align_bytes=64)
+            for o in range(PASSES):
+                score_pass(g, b, o)
+            silu[g, b] = keep.tile([P, P, PACK], F32, name=f"silu{g}_{b}", tag=f"silu{g}_{b}", align_bytes=64)
             nc.scalar.activation(silu[g, b][:], score[g, b][:].rearrange("p t q -> p q t"), ACT.Silu)
 
         y = [psum.tile([P, DV], F32, name=f"y{b}", tag=f"score{PAGES - 1}_{b}") for b in range(QBLOCKS)]
 
         def scale(g, b):
-            if (g, b) == (0, 0):
-                w_bf = shared.tile([P, P, PACK], BF16, name="w_bf0_0", align_bytes=64, offset=ROW_BYTES + 1024)
-            else:
-                w_bf = keep.tile([P, P, PACK], BF16, name=f"w_bf{g}_{b}", align_bytes=64)
+            w_bf = keep.tile([P, P, PACK], BF16, name=f"w_bf{g}_{b}", align_bytes=64)
             nc.vector.tensor_tensor(w_bf[:], silu[g, b][:], vs_col[g].unsqueeze(1).to_broadcast([P, P, PACK]), MULT)
             return w_bf
 
-        def multiply(g, b, w_bf):
+        def quantise_weights(g, b, w_bf):
             w_codes = keep.tile([P, P], U32, name=f"w_codes{g}_{b}", align_bytes=64)
             w_scales = keep.tile([P, P], U8, name=f"w_scales{g}_{b}", align_bytes=64)
             nc.vector.quantize_mx(
                 out=w_codes[:].bitcast(FP8X4), scales=w_scales[:], in_=w_bf[:].rearrange("p q t -> p (q t)")
             )
+            return g, b, w_codes, w_scales
+
+        def multiply(g, b, w_codes, w_scales):
             nc.tensor.matmul_mx(
                 out=y[b][:],
                 lhsT=w_codes[:].bitcast(FP8X4),
@@ -217,9 +233,12 @@ def tile_attend_pkv4_silu_kernel(tc, qT, k_words, k_scales, v_words, v_scales, v
                 queue.dma_start(out[0, b * P : (b + 1) * P, :], result[:])
 
         pending = None
+        quantised = []
         for g, b in chunks:
             w_bf = scale(g, b)
             if pending is not None:
-                multiply(*pending)
+                quantised.append(quantise_weights(*pending))
             pending = (g, b, w_bf)
-        multiply(*pending)
+        quantised.append(quantise_weights(*pending))
+        for item in quantised:
+            multiply(*item)

@@ -1,6 +1,7 @@
 from contextlib import ExitStack
 
 import concourse.mybir as mybir
+from concourse.masks import make_identity
 
 N, T, D, DV, NQ = 1536, 4096, 1024, 128, 256
 PAGE = 512
@@ -28,6 +29,8 @@ VS_ROW = P - 1
 KS_ROW = 32
 VSC_ROW = P - 16
 ODD_SPLIT = T // 8 + 1
+VS_SHARE = 600
+TURNED = 2
 ROW_BYTES = 4 * PACK * NQ
 Q0_AT = 3 * ROW_BYTES
 KS_AT = 4 * ROW_BYTES
@@ -65,11 +68,15 @@ def tile_attend_pkv4_silu_kernel(tc, qT, k_words, k_scales, v_words, v_scales, v
         for rows in (slice(0, KS_ROW), slice(KS_ROW + 32, P)):
             for cols in (slice(0, ODD_SPLIT), slice(ODD_SPLIT, T // 4)):
                 nc.vector.memset(ks_pool[rows, cols], 0)
+        for cols in (slice(0, VS_SHARE // 2 + 1), slice(VS_SHARE // 2 + 1, VS_SHARE)):
+            nc.vector.memset(vs_pool[0:VS_ROW, cols].bitcast(I32), 0)
 
         warm = keep.tile([P, 1], F32, name="warm")
         nc.gpsimd.memset(warm[:], 0.0)
+        nc.gpsimd.memset(vs_pool[0:VS_ROW, VS_SHARE:T].bitcast(I32), 0)
         nc.gpsimd.memset(vsc_pool[0:VSC_ROW, :], 0)
-        nc.gpsimd.memset(vs_pool[0:VS_ROW, :].bitcast(I32), 0)
+        ident = keep.tile([P, P], F32, name="ident", align_bytes=64)
+        make_identity(nc, ident[:])
         warmed = keep.tile([P, 1], F32, name="warmed")
         nc.scalar.activation(warmed[:], warm[:], ACT.Silu)
 
@@ -153,7 +160,14 @@ def tile_attend_pkv4_silu_kernel(tc, qT, k_words, k_scales, v_words, v_scales, v
             v_words.rearrange("u g e r -> g u (e r)").bitcast(I32),
         )
         place_planes(1, PAGES - 1)
-        vs_col = [place_column(g) for g in range(PAGES)]
+        vs_bank = psum.tile([P, PAGE], F32, name="vs_bank")
+        vs_col = []
+        for g in range(TURNED):
+            first = 2 * PACK * (TURNED - 1 - g)
+            for t in reversed(range(PACK)):
+                nc.tensor.transpose(vs_bank[:, first + 2 * t : first + 2 * t + P], vs_got[g][:, t:PAGE:PACK], ident[:])
+            vs_col.append(vs_bank[:, first + VS_ROW : first + VS_ROW + 2 * PACK : 2])
+        vs_col.extend(place_column(g) for g in range(TURNED, PAGES))
         for o in range(PASSES):
             for b in range(QBLOCKS):
                 cast_queries(o, b)

@@ -30,10 +30,16 @@ KS_ROW = 32
 VSC_ROW = P - 16
 ODD_SPLIT = T // 8 + 1
 VS_SHARE = 600
-TURNED = 2
-ROW_BYTES = 4 * PACK * NQ
-Q0_AT = 3 * ROW_BYTES
-KS_AT = 4 * ROW_BYTES
+RAW_BYTES = 4 * PACK * P
+KEY_BYTES = 2 * PAGE
+EARLY = 2
+SILU_AT = 512
+Q_AT = {(1, 1): 2 * RAW_BYTES, (0, 0): 5 * RAW_BYTES, (0, 1): 6 * RAW_BYTES, (1, 0): 7 * RAW_BYTES + KEY_BYTES}
+KS_GOT_AT = 3 * RAW_BYTES - 64
+VW_AT = 3 * RAW_BYTES
+GOT2_AT = Q_AT[0, 1] + KEY_BYTES
+KS_AT = Q_AT[1, 0] + RAW_BYTES
+KEYS_AT = {(1, 0): Q_AT[0, 0], (1, 1): Q_AT[0, 1], (2, 0): Q_AT[1, 0], (2, 1): SILU_AT + EARLY * RAW_BYTES}
 
 
 def tile_attend_pkv4_silu_kernel(tc, qT, k_words, k_scales, v_words, v_scales, vs, offs, voffs, out):
@@ -56,14 +62,18 @@ def tile_attend_pkv4_silu_kernel(tc, qT, k_words, k_scales, v_words, v_scales, v
             vsc_pool[VSC_ROW:P, :].rearrange("f (u e) -> f u e", u=POOL_PAGES),
             v_scales.bitcast(I32).rearrange("u f e -> f u e"),
         )
-        q_rows = qT[0].rearrange("(o p j) q -> o p (j q)", o=PASSES, j=PACK)
+        q_rows = qT[0].rearrange("(o p j) (b q) -> b o p j q", o=PASSES, j=PACK, b=QBLOCKS)
+        q_raw = {}
+
+        def load_queries(b, o):
+            q_raw[b, o] = shared.tile([P, PACK, P], F32, name=f"q_raw{b}_{o}", align_bytes=64, offset=Q_AT[b, o])
+            nc.sync.dma_start(q_raw[b, o][:], q_rows[b, o])
+
         kw_pool = keep.tile([P, T], I32, name="kw_pool", align_bytes=64)
         nc.sync.dma_start(kw_pool[:], k_words[0].rearrange("g t b -> g (t b)").bitcast(I32))
-        q_raw0 = shared.tile([P, PACK * NQ], F32, name="q_raw0", align_bytes=64, offset=Q0_AT)
-        nc.sync.dma_start(q_raw0[:], q_rows[0])
-        q_raw1 = shared.tile([P, PACK * NQ], F32, name="q_raw1", align_bytes=64, offset=0)
-        nc.sync.dma_start(q_raw1[:], q_rows[1])
-        q_raw = [q_raw0, q_raw1]
+        load_queries(0, 0)
+        load_queries(0, 1)
+        load_queries(1, 0)
 
         for rows in (slice(0, KS_ROW), slice(KS_ROW + 32, P)):
             for cols in (slice(0, ODD_SPLIT), slice(ODD_SPLIT, T // 4)):
@@ -80,7 +90,7 @@ def tile_attend_pkv4_silu_kernel(tc, qT, k_words, k_scales, v_words, v_scales, v
         warmed = keep.tile([P, 1], F32, name="warmed")
         nc.scalar.activation(warmed[:], warm[:], ACT.Silu)
 
-        ks_got = shared.tile([P, N], U8, name="ks_got", align_bytes=64, offset=ROW_BYTES)
+        ks_got = shared.tile([P, N], U8, name="ks_got", align_bytes=64, offset=KS_GOT_AT)
         nc.vector.tensor_copy(ks_got[:], ks_pool[:].bitcast(U8).indirect(offs_sb[:]))
         vsc_got = keep.tile([P, PAGES * DV], U8, name="vsc_got", align_bytes=64)
         nc.vector.tensor_copy(vsc_got[:], vsc_pool[:].bitcast(U8).indirect(voffs_sb[:]))
@@ -89,45 +99,43 @@ def tile_attend_pkv4_silu_kernel(tc, qT, k_words, k_scales, v_words, v_scales, v
             ks_dealt[:].bitcast(U8).rearrange("p (g h t s) -> p h g t s", g=PAGES, h=2, t=PACK // 2),
             ks_got[:].rearrange("p (g s h t) -> p h g t s", g=PAGES, h=2, t=PACK // 2),
         )
+        planes = shared.tile([P, PASSES * N // 4], I32, name="planes", align_bytes=64, offset=KS_AT)
+        for c in (0, 2, 1, 3):
+            nc.sync.dma_start(planes[32 * c : 32 * c + 4, :], ks_dealt[KS_ROW + 8 * c : KS_ROW + 8 * c + 8, :])
         ks_plane = {}
-
-        def place_planes(first, count):
-            words = count * PAGE // 4
-            planes = shared.tile([P, PASSES * words], I32, name=f"planes{first}", align_bytes=64, offset=KS_AT + PASSES * PAGE * first)
-            for c in (0, 2, 1, 3):
-                rows = slice(KS_ROW + 8 * c, KS_ROW + 8 * c + 8)
-                nc.sync.dma_start(planes[32 * c : 32 * c + 4, :], ks_dealt[rows, first * PAGE // 4 : first * PAGE // 4 + words])
-            for g in range(count):
-                for o in range(PASSES):
-                    at = (o * count + g) * PAGE
-                    ks_plane[first + g, o] = planes[:].bitcast(U8)[:, at : at + PAGE]
-
-        place_planes(0, 1)
+        for g in range(PAGES):
+            for o in range(PASSES):
+                ks_plane[g, o] = planes[:].bitcast(U8)[:, o * N + g * PAGE : o * N + (g + 1) * PAGE]
+        load_queries(1, 1)
+        vw_pool = shared.tile([P, POOL_PAGES * DV], I32, name="vw_pool", align_bytes=64, offset=VW_AT)
+        nc.sync.dma_start(
+            vw_pool[:].rearrange("g (u e) -> g u e", u=POOL_PAGES),
+            v_words.rearrange("u g e r -> g u (e r)").bitcast(I32),
+        )
 
         q_codes = keep.tile([P, QBLOCKS * PASSES * P], U32, name="q_codes", align_bytes=64)
         q_scales = keep.tile([P, QBLOCKS * PASSES * P], U8, name="q_scales", align_bytes=64)
 
         q_bf = keep.tile([P, QBLOCKS * PASSES * P * PACK], BF16, name="q_bf", tag="q_bf", align_bytes=64)
 
-        def cast_queries(o, b):
+        def cast_queries(b, o):
             at = (b * PASSES + o) * P * PACK
-            rows = q_raw[o][:].rearrange("p (j q) -> p j q", j=PACK)[:, :, b * P : (b + 1) * P]
             nc.scalar.copy(
                 q_bf[:, at : at + P * PACK].rearrange("p (c i j) -> p c j i", i=4, j=PACK),
-                rows.rearrange("p j (c i) -> p c j i", i=4),
+                q_raw[b, o][:].rearrange("p j (c i) -> p c j i", i=4),
             )
 
-        def quantise_queries(first, count):
-            cols = slice(first * P, (first + count) * P)
+        def quantise_queries(b, o):
+            at = (b * PASSES + o) * P
             nc.vector.quantize_mx(
-                out=q_codes[:, cols].bitcast(FP8X4),
-                scales=q_scales[:, cols],
-                in_=q_bf[:, first * P * PACK : (first + count) * P * PACK],
+                out=q_codes[:, at : at + P].bitcast(FP8X4),
+                scales=q_scales[:, at : at + P],
+                in_=q_bf[:, at * PACK : (at + P) * PACK],
             )
 
         def gather_keys(g):
             if g == PAGES - 1:
-                kw_got = shared.tile([P, PAGE], U32, name=f"kw_got{g}", align_bytes=64, offset=Q0_AT)
+                kw_got = shared.tile([P, PAGE], U32, name=f"kw_got{g}", align_bytes=64, offset=GOT2_AT)
             else:
                 kw_got = keep.tile([P, PAGE], U32, name=f"kw_got{g}", tag=f"got{g}", align_bytes=64)
             nc.vector.tensor_copy(kw_got[:], kw_pool[:].bitcast(U32).indirect(offs_sb[:, g * LIST_COLS : (g + 1) * LIST_COLS]))
@@ -135,13 +143,14 @@ def tile_attend_pkv4_silu_kernel(tc, qT, k_words, k_scales, v_words, v_scales, v
 
         keys = {}
 
-        def part_keys(g, o, kw_got, tile):
+        def part_keys(g, o, kw_got):
+            if (g, o) in KEYS_AT:
+                tile = shared.tile([P, KEY_BYTES], U8, name=f"keys{g}_{o}", align_bytes=64, offset=KEYS_AT[g, o])
+            else:
+                tile = keep.tile([P, KEY_BYTES], U8, name=f"keys{g}_{o}", align_bytes=64)
             halves = kw_got[:].bitcast(U16).rearrange("p (c i t o) -> p o c t i", i=4, t=PACK, o=PASSES)
             nc.vector.tensor_copy(tile[:].bitcast(U16).rearrange("p (t c i) -> p c t i", t=PACK, i=4), halves[:, o])
             keys[g, o] = tile
-
-        def key_tile(g, o):
-            return keep.tile([P, 2 * PAGE], U8, name=f"keys{g}_{o}", align_bytes=64)
 
         vs_got = []
         for g in range(PAGES):
@@ -149,40 +158,29 @@ def tile_attend_pkv4_silu_kernel(tc, qT, k_words, k_scales, v_words, v_scales, v
             nc.scalar.activation(got[:], vs_pool[:].indirect(offs_sb[:, g * LIST_COLS : (g + 1) * LIST_COLS]), ACT.Copy)
             vs_got.append(got)
 
-        def place_column(g):
-            col = shared.tile([P, PACK], F32, name=f"vs_col{g}", offset=ROW_BYTES + 32 * g)
-            nc.sync.dma_start(col[:], vs_got[g][VS_ROW:P, :])
-            return col[:]
-
-        vw_pool = shared.tile([P, POOL_PAGES * DV], I32, name="vw_pool", align_bytes=64, offset=ROW_BYTES + 128)
-        nc.sync.dma_start(
-            vw_pool[:].rearrange("g (u e) -> g u e", u=POOL_PAGES),
-            v_words.rearrange("u g e r -> g u (e r)").bitcast(I32),
-        )
-        place_planes(1, PAGES - 1)
         vs_bank = psum.tile([P, PAGE], F32, name="vs_bank")
         vs_col = []
-        for g in range(TURNED):
-            first = 2 * PACK * (TURNED - 1 - g)
+        for g in range(PAGES):
+            first = 2 * PACK * (PAGES - 1 - g)
             for t in reversed(range(PACK)):
                 nc.tensor.transpose(vs_bank[:, first + 2 * t : first + 2 * t + P], vs_got[g][:, t:PAGE:PACK], ident[:])
             vs_col.append(vs_bank[:, first + VS_ROW : first + VS_ROW + 2 * PACK : 2])
-        vs_col.extend(place_column(g) for g in range(TURNED, PAGES))
-        for o in range(PASSES):
-            for b in range(QBLOCKS):
-                cast_queries(o, b)
+        for b in range(QBLOCKS):
+            for o in range(PASSES):
+                cast_queries(b, o)
         got0 = gather_keys(0)
         got1 = gather_keys(1)
-        part_keys(0, 0, got0, key_tile(0, 0))
-        part_keys(0, 1, got0, key_tile(0, 1))
+        part_keys(0, 0, got0)
+        part_keys(0, 1, got0)
+        quantise_queries(0, 0)
+        part_keys(1, 0, got1)
         quantise_queries(0, 1)
         got2 = gather_keys(2)
+        part_keys(1, 1, got1)
+        quantise_queries(1, 0)
+        part_keys(2, 0, got2)
         quantise_queries(1, 1)
-        part_keys(1, 0, got1, shared.tile([P, 2 * PAGE], U8, name="keys1_0", align_bytes=64, offset=Q0_AT + 4 * PAGE))
-        quantise_queries(PASSES, PASSES)
-        for slot, (g, o, got) in enumerate(((1, 1, got1), (2, 0, got2), (2, 1, got2))):
-            tile = shared.tile([P, 2 * PAGE], U8, name=f"keys{g}_{o}", align_bytes=64, offset=2 * PAGE * slot)
-            part_keys(g, o, got, tile)
+        part_keys(2, 1, got2)
         vw_got = keep.tile([P, PAGES * DV], U32, name="vw_got", tag="q_bf", align_bytes=64)
         nc.vector.tensor_copy(vw_got[:], vw_pool[:].bitcast(U32).indirect(voffs_sb[:]))
 
@@ -191,7 +189,7 @@ def tile_attend_pkv4_silu_kernel(tc, qT, k_words, k_scales, v_words, v_scales, v
         for c in range(4):
             nc.sync.dma_start(vsc_words[32 * c : 32 * c + 4, :], vsc_got[:].bitcast(I32)[VSC_ROW + 4 * c : VSC_ROW + 4 * c + 4, :])
 
-        chunks = [(g, b) for g in range(PAGES) for b in range(QBLOCKS)]
+        chunks = [(g, b) for b in range(QBLOCKS) for g in range(PAGES - 1)] + [(PAGES - 1, b) for b in range(QBLOCKS)]
         score = {}
         for g, b in chunks:
             score[g, b] = psum.tile([P, PACK, P], F32, name=f"score{g}_{b}", tag=f"score{g}_{b}")
@@ -209,17 +207,21 @@ def tile_attend_pkv4_silu_kernel(tc, qT, k_words, k_scales, v_words, v_scales, v
                 )
 
         silu = {}
-        for g, b in chunks:
+        early_silu = shared.tile([P, EARLY, P, PACK], F32, name="early_silu", align_bytes=64, offset=SILU_AT)
+        for n, (g, b) in enumerate(chunks):
             for o in range(PASSES):
                 score_pass(g, b, o)
-            silu[g, b] = keep.tile([P, P, PACK], F32, name=f"silu{g}_{b}", tag=f"silu{g}_{b}", align_bytes=64)
-            nc.scalar.activation(silu[g, b][:], score[g, b][:].rearrange("p t q -> p q t"), ACT.Silu)
+            if n < EARLY:
+                silu[g, b] = early_silu[:, n]
+            else:
+                silu[g, b] = keep.tile([P, P, PACK], F32, name=f"silu{g}_{b}", align_bytes=64)[:]
+            nc.scalar.activation(silu[g, b], score[g, b][:].rearrange("p t q -> p q t"), ACT.Silu)
 
         y = [psum.tile([P, DV], F32, name=f"y{b}", tag=f"score{PAGES - 1}_{b}") for b in range(QBLOCKS)]
 
         def scale(g, b):
             w_bf = keep.tile([P, P, PACK], BF16, name=f"w_bf{g}_{b}", align_bytes=64)
-            nc.vector.tensor_tensor(w_bf[:], silu[g, b][:], vs_col[g].unsqueeze(1).to_broadcast([P, P, PACK]), MULT)
+            nc.vector.tensor_tensor(w_bf[:], silu[g, b], vs_col[g].unsqueeze(1).to_broadcast([P, P, PACK]), MULT)
             return w_bf
 
         def quantise_weights(g, b, w_bf):

@@ -29,10 +29,10 @@ VS_ROW = P - 1
 KS_ROW = 32
 VSC_ROW = P - 16
 ODD_SPLIT = T // 8 + 1
-VS_SHARE = 600
 RAW_BYTES = 4 * PACK * P
 KEY_BYTES = 2 * PAGE
 EARLY = 2
+VS_FIRST = 256
 SILU_AT = 512
 Q_AT = {(1, 1): 2 * RAW_BYTES, (0, 0): 5 * RAW_BYTES, (0, 1): 6 * RAW_BYTES, (1, 0): 7 * RAW_BYTES + KEY_BYTES}
 KS_GOT_AT = 3 * RAW_BYTES - 64
@@ -78,17 +78,16 @@ def tile_attend_pkv4_silu_kernel(tc, qT, k_words, k_scales, v_words, v_scales, v
         for rows in (slice(0, KS_ROW), slice(KS_ROW + 32, P)):
             for cols in (slice(0, ODD_SPLIT), slice(ODD_SPLIT, T // 4)):
                 nc.vector.memset(ks_pool[rows, cols], 0)
-        for cols in (slice(0, VS_SHARE // 2 + 1), slice(VS_SHARE // 2 + 1, VS_SHARE)):
-            nc.vector.memset(vs_pool[0:VS_ROW, cols].bitcast(I32), 0)
+        for cols in (slice(0, DV + 1), slice(DV + 1, 2 * DV)):
+            nc.vector.memset(vsc_pool[0:VSC_ROW, cols], 0)
 
-        warm = keep.tile([P, 1], F32, name="warm")
-        nc.gpsimd.memset(warm[:], 0.0)
-        nc.gpsimd.memset(vs_pool[0:VS_ROW, VS_SHARE:T].bitcast(I32), 0)
-        nc.gpsimd.memset(vsc_pool[0:VSC_ROW, :], 0)
         ident = keep.tile([P, P], F32, name="ident", align_bytes=64)
-        make_identity(nc, ident[:])
+        nc.gpsimd.memset(ident[:], 0.0)
+        nc.gpsimd.memset(vs_pool[0:VS_ROW, 0:VS_FIRST].bitcast(I32), 0)
+        make_identity(nc, ident[:], nomemset=True)
+        nc.gpsimd.memset(vs_pool[0:VS_ROW, VS_FIRST:T].bitcast(I32), 0)
         warmed = keep.tile([P, 1], F32, name="warmed")
-        nc.scalar.activation(warmed[:], warm[:], ACT.Silu)
+        nc.scalar.activation(warmed[:], ident[:, 0:1], ACT.Silu)
 
         ks_got = shared.tile([P, N], U8, name="ks_got", align_bytes=64, offset=KS_GOT_AT)
         nc.vector.tensor_copy(ks_got[:], ks_pool[:].bitcast(U8).indirect(offs_sb[:]))
@@ -189,7 +188,7 @@ def tile_attend_pkv4_silu_kernel(tc, qT, k_words, k_scales, v_words, v_scales, v
         for c in range(4):
             nc.sync.dma_start(vsc_words[32 * c : 32 * c + 4, :], vsc_got[:].bitcast(I32)[VSC_ROW + 4 * c : VSC_ROW + 4 * c + 4, :])
 
-        chunks = [(g, b) for b in range(QBLOCKS) for g in range(PAGES - 1)] + [(PAGES - 1, b) for b in range(QBLOCKS)]
+        chunks = [(0, 0), (1, 0), (0, 1), (2, 0), (1, 1), (2, 1)]
         score = {}
         for g, b in chunks:
             score[g, b] = psum.tile([P, PACK, P], F32, name=f"score{g}_{b}", tag=f"score{g}_{b}")

@@ -65,15 +65,17 @@ def tile_attend_pkv4_silu_kernel(tc, qT, k_words, k_scales, v_words, v_scales, v
         q_rows = qT[0].rearrange("(o p j) (b q) -> b o p j q", o=PASSES, j=PACK, b=QBLOCKS)
         q_raw = {}
 
-        def load_queries(b, o):
+        def load_queries(b, o, pieces=1):
             q_raw[b, o] = shared.tile([P, PACK, P], F32, name=f"q_raw{b}_{o}", align_bytes=64, offset=Q_AT[b, o])
-            nc.sync.dma_start(q_raw[b, o][:], q_rows[b, o])
+            rows = PACK // pieces
+            for j in range(0, PACK, rows):
+                nc.sync.dma_start(q_raw[b, o][:, j : j + rows, :], q_rows[b, o][:, j : j + rows, :])
 
         kw_pool = keep.tile([P, T], I32, name="kw_pool", align_bytes=64)
         nc.sync.dma_start(kw_pool[:], k_words[0].rearrange("g t b -> g (t b)").bitcast(I32))
         load_queries(0, 0)
         load_queries(0, 1)
-        load_queries(1, 0)
+        load_queries(1, 0, pieces=2)
 
         for rows in (slice(0, KS_ROW), slice(KS_ROW + 32, P)):
             for cols in (slice(0, ODD_SPLIT), slice(ODD_SPLIT, T // 4)):

@@ -32,13 +32,16 @@ ODD_SPLIT = T // 8 + 1
 RAW_BYTES = 4 * PACK * P
 KEY_BYTES = 2 * PAGE
 EARLY = 2
-VS_FIRST = 256
+VS_SPREAD = 1856
+ROW = 256
+KS_PIECES = ((0, PAGES - 1), (PAGES - 1, 1))
 SILU_AT = 512
 Q_AT = {(1, 1): 2 * RAW_BYTES, (0, 0): 5 * RAW_BYTES, (0, 1): 6 * RAW_BYTES, (1, 0): 7 * RAW_BYTES + KEY_BYTES}
 KS_GOT_AT = 3 * RAW_BYTES - 64
 VW_AT = 3 * RAW_BYTES
 GOT2_AT = Q_AT[0, 1] + KEY_BYTES
 KS_AT = Q_AT[1, 0] + RAW_BYTES
+VS_AT = KS_AT + T
 KEYS_AT = {(1, 0): Q_AT[0, 0], (1, 1): Q_AT[0, 1], (2, 0): Q_AT[1, 0], (2, 1): SILU_AT + EARLY * RAW_BYTES}
 
 
@@ -49,75 +52,103 @@ def tile_attend_pkv4_silu_kernel(tc, qT, k_words, k_scales, v_words, v_scales, v
         shared = ctx.enter_context(tc.tile_pool(name="shared", bufs=1))
         psum = ctx.enter_context(tc.psum_pool(name="psum", bufs=1))
 
-        offs_sb = keep.tile([P, N // 16], U16, name="offs_sb")
-        nc.sync.dma_start(offs_sb[:], offs)
-        ks_pool = shared.tile([P, T // 4], I32, name="ks_pool", align_bytes=64, offset=KS_AT)
-        nc.sync.dma_start(ks_pool[KS_ROW : KS_ROW + 32, :], k_scales.bitcast(I32).rearrange("o f t -> f o t"))
-        vs_pool = keep.tile([P, T], F32, name="vs_pool", align_bytes=64)
-        nc.sync.dma_start(vs_pool[VS_ROW:P, :], vs[0:1, :])
         voffs_sb = keep.tile([P, PAGES * DV // 16], U16, name="voffs_sb")
         nc.sync.dma_start(voffs_sb[:], voffs)
-        vsc_pool = keep.tile([P, POOL_PAGES * DV // 4], I32, name="vsc_pool", align_bytes=64)
-        nc.sync.dma_start(
+        vsc_pool = keep.tile([P, POOL_PAGES * DV // 4], I32, name="vsc_pool", align_bytes=ROW)
+        nc.scalar.dma_start(
             vsc_pool[VSC_ROW:P, :].rearrange("f (u e) -> f u e", u=POOL_PAGES),
             v_scales.bitcast(I32).rearrange("u f e -> f u e"),
         )
+        ks_pool = shared.tile([P, T // 4], I32, name="ks_pool", align_bytes=ROW, offset=KS_AT)
+        nc.sync.dma_start(ks_pool[KS_ROW : KS_ROW + 32, :], k_scales.bitcast(I32).rearrange("o (h a) t -> a (o h) t", h=2))
+        vs_pool = shared.tile([P, T], F32, name="vs_pool", align_bytes=ROW, offset=VS_AT)
+        nc.scalar.dma_start(vs_pool[VS_ROW:P, :], vs[0:1, :])
+        offs_sb = keep.tile([P, N // 16], U16, name="offs_sb")
+        nc.sync.dma_start(offs_sb[:], offs)
         q_rows = qT[0].rearrange("(o p j) (b q) -> b o p j q", o=PASSES, j=PACK, b=QBLOCKS)
         q_raw = {}
 
         def load_queries(b, o, pieces=1):
-            q_raw[b, o] = shared.tile([P, PACK, P], F32, name=f"q_raw{b}_{o}", align_bytes=64, offset=Q_AT[b, o])
+            q_raw[b, o] = shared.tile([P, PACK, P], F32, name=f"q_raw{b}_{o}", align_bytes=ROW, offset=Q_AT[b, o])
             rows = PACK // pieces
             for j in range(0, PACK, rows):
                 nc.sync.dma_start(q_raw[b, o][:, j : j + rows, :], q_rows[b, o][:, j : j + rows, :])
 
-        kw_pool = keep.tile([P, T], I32, name="kw_pool", align_bytes=64)
+        kw_pool = keep.tile([P, T], I32, name="kw_pool", align_bytes=ROW)
         nc.sync.dma_start(kw_pool[:], k_words[0].rearrange("g t b -> g (t b)").bitcast(I32))
         load_queries(0, 0)
         load_queries(0, 1)
         load_queries(1, 0, pieces=2)
 
-        for rows in (slice(0, KS_ROW), slice(KS_ROW + 32, P)):
-            for cols in (slice(0, ODD_SPLIT), slice(ODD_SPLIT, T // 4)):
-                nc.vector.memset(ks_pool[rows, cols], 0)
-        for cols in (slice(0, DV + 1), slice(DV + 1, 2 * DV)):
-            nc.vector.memset(vsc_pool[0:VSC_ROW, cols], 0)
+        warm_in = keep.tile([P, 1], F32, name="warm_in")
+        nc.vector.memset(warm_in[:], 0.0)
+        nc.vector.memset(vs_pool[0:VS_ROW, 0:1].bitcast(I32), 0)
+        for cols in (slice(0, ODD_SPLIT), slice(ODD_SPLIT, T // 4)):
+            nc.vector.memset(ks_pool[KS_ROW + 32 : P, cols], 0)
 
         ident = keep.tile([P, P], F32, name="ident", align_bytes=64)
         nc.gpsimd.memset(ident[:], 0.0)
-        nc.gpsimd.memset(vs_pool[0:VS_ROW, 0:VS_FIRST].bitcast(I32), 0)
+        nc.gpsimd.memset(vsc_pool[0:VSC_ROW, :], 0)
+        nc.gpsimd.memset(ks_pool[0:KS_ROW, :], 0)
         make_identity(nc, ident[:], nomemset=True)
-        nc.gpsimd.memset(vs_pool[0:VS_ROW, VS_FIRST:T].bitcast(I32), 0)
+        nc.gpsimd.memset(vs_pool[0:VS_ROW, VS_SPREAD:T].bitcast(I32), 0)
         warmed = keep.tile([P, 1], F32, name="warmed")
-        nc.scalar.activation(warmed[:], ident[:, 0:1], ACT.Silu)
+        nc.scalar.activation(warmed[:], warm_in[:], ACT.Silu)
+        nc.scalar.activation(
+            vs_pool[0:VS_ROW, 1:VS_SPREAD], vs_pool[0:VS_ROW, 0:1].to_broadcast([VS_ROW, VS_SPREAD - 1]), ACT.Copy
+        )
 
-        ks_got = shared.tile([P, N], U8, name="ks_got", align_bytes=64, offset=KS_GOT_AT)
-        nc.vector.tensor_copy(ks_got[:], ks_pool[:].bitcast(U8).indirect(offs_sb[:]))
         vsc_got = keep.tile([P, PAGES * DV], U8, name="vsc_got", align_bytes=64)
         nc.vector.tensor_copy(vsc_got[:], vsc_pool[:].bitcast(U8).indirect(voffs_sb[:]))
-        ks_dealt = keep.tile([P, N // 4], I32, name="ks_dealt", align_bytes=64)
-        nc.vector.tensor_copy(
-            ks_dealt[:].bitcast(U8).rearrange("p (g h t s) -> p h g t s", g=PAGES, h=2, t=PACK // 2),
-            ks_got[:].rearrange("p (g s h t) -> p h g t s", g=PAGES, h=2, t=PACK // 2),
-        )
-        planes = shared.tile([P, PASSES * N // 4], I32, name="planes", align_bytes=64, offset=KS_AT)
+        ks_got = []
+        for first, count in KS_PIECES:
+            if first == 0:
+                got = keep.tile([P, count * PAGE], U8, name=f"ks_got{first}", align_bytes=64)
+            else:
+                got = shared.tile([P, count * PAGE], U8, name=f"ks_got{first}", align_bytes=64, offset=KS_GOT_AT)
+            listed = offs_sb[:, first * LIST_COLS : (first + count) * LIST_COLS]
+            nc.vector.tensor_copy(got[:], ks_pool[:].bitcast(U8).indirect(listed))
+            ks_got.append(got)
+        ks_dealt = keep.tile([P, N // 4], I32, name="ks_dealt", align_bytes=ROW)
+        for (first, count), got in zip(KS_PIECES, ks_got):
+            dealt = ks_dealt[:].bitcast(U8)[:, first * PAGE : (first + count) * PAGE]
+            nc.vector.tensor_copy(
+                dealt.rearrange("p (g h t s) -> p h g t s", g=count, h=2, t=PACK // 2),
+                got[:].rearrange("p (g s h t) -> p h g t s", g=count, h=2, t=PACK // 2),
+            )
+        planes = shared.tile([P, PASSES * N // 4], I32, name="planes", align_bytes=ROW, offset=KS_AT)
         for c in (0, 2, 1, 3):
-            nc.sync.dma_start(planes[32 * c : 32 * c + 4, :], ks_dealt[KS_ROW + 8 * c : KS_ROW + 8 * c + 8, :])
+            first = KS_ROW + 16 * (c % 2) + c // 2
+            nc.sync.dma_start(planes[32 * c : 32 * c + 4, :], ks_dealt[first : first + 15 : 2, :])
         ks_plane = {}
         for g in range(PAGES):
             for o in range(PASSES):
                 ks_plane[g, o] = planes[:].bitcast(U8)[:, o * N + g * PAGE : o * N + (g + 1) * PAGE]
         load_queries(1, 1)
-        vw_pool = shared.tile([P, POOL_PAGES * DV], I32, name="vw_pool", align_bytes=64, offset=VW_AT)
+        vw_pool = shared.tile([P, POOL_PAGES * DV], I32, name="vw_pool", align_bytes=ROW, offset=VW_AT)
         nc.sync.dma_start(
             vw_pool[:].rearrange("g (u e) -> g u e", u=POOL_PAGES),
             v_words.rearrange("u g e r -> g u (e r)").bitcast(I32),
         )
 
+        vs_got = []
+        for g in range(PAGES):
+            got = keep.tile([P, PAGE], F32, name=f"vs_got{g}", align_bytes=64)
+            nc.scalar.activation(got[:], vs_pool[:].indirect(offs_sb[:, g * LIST_COLS : (g + 1) * LIST_COLS]), ACT.Copy)
+            vs_got.append(got)
+
+        vs_bank = psum.tile([P, PAGE], F32, name="vs_bank")
+        vs_col = []
+        for g in range(PAGES):
+            first = 2 * PACK * (PAGES - 1 - g)
+            for t in reversed(range(PACK)):
+                nc.tensor.transpose(vs_bank[:, first + 2 * t : first + 2 * t + P], vs_got[g][:, t:PAGE:PACK], ident[:])
+            vs_col.append(vs_bank[:, first + VS_ROW : first + VS_ROW + 2 * PACK : 2])
+
         q_codes = keep.tile([P, QBLOCKS * PASSES * P], U32, name="q_codes", align_bytes=64)
         q_scales = keep.tile([P, QBLOCKS * PASSES * P], U8, name="q_scales", align_bytes=64)
 
-        q_bf = keep.tile([P, QBLOCKS * PASSES * P * PACK], BF16, name="q_bf", tag="q_bf", align_bytes=64)
+        q_bf = shared.tile([P, QBLOCKS * PASSES * P * PACK], BF16, name="q_bf", align_bytes=64, offset=VS_AT)
 
         def cast_queries(b, o):
             at = (b * PASSES + o) * P * PACK
@@ -153,19 +184,6 @@ def tile_attend_pkv4_silu_kernel(tc, qT, k_words, k_scales, v_words, v_scales, v
             nc.vector.tensor_copy(tile[:].bitcast(U16).rearrange("p (t c i) -> p c t i", t=PACK, i=4), halves[:, o])
             keys[g, o] = tile
 
-        vs_got = []
-        for g in range(PAGES):
-            got = keep.tile([P, PAGE], F32, name=f"vs_got{g}", align_bytes=64)
-            nc.scalar.activation(got[:], vs_pool[:].indirect(offs_sb[:, g * LIST_COLS : (g + 1) * LIST_COLS]), ACT.Copy)
-            vs_got.append(got)
-
-        vs_bank = psum.tile([P, PAGE], F32, name="vs_bank")
-        vs_col = []
-        for g in range(PAGES):
-            first = 2 * PACK * (PAGES - 1 - g)
-            for t in reversed(range(PACK)):
-                nc.tensor.transpose(vs_bank[:, first + 2 * t : first + 2 * t + P], vs_got[g][:, t:PAGE:PACK], ident[:])
-            vs_col.append(vs_bank[:, first + VS_ROW : first + VS_ROW + 2 * PACK : 2])
         for b in range(QBLOCKS):
             for o in range(PASSES):
                 cast_queries(b, o)
@@ -182,7 +200,7 @@ def tile_attend_pkv4_silu_kernel(tc, qT, k_words, k_scales, v_words, v_scales, v
         part_keys(2, 0, got2)
         quantise_queries(1, 1)
         part_keys(2, 1, got2)
-        vw_got = keep.tile([P, PAGES * DV], U32, name="vw_got", tag="q_bf", align_bytes=64)
+        vw_got = shared.tile([P, PAGES * DV], U32, name="vw_got", align_bytes=64, offset=VS_AT)
         nc.vector.tensor_copy(vw_got[:], vw_pool[:].bitcast(U32).indirect(voffs_sb[:]))
 
         vsc_words = keep.tile([P, PAGES * DV // 4], I32, name="vsc_words", tag="got0", align_bytes=64)
@@ -244,7 +262,7 @@ def tile_attend_pkv4_silu_kernel(tc, qT, k_words, k_scales, v_words, v_scales, v
                 stop=(g == PAGES - 1),
             )
             if g == PAGES - 1:
-                result = keep.tile([P, DV], F32, name=f"result{b}")
+                result = keep.tile([P, DV], F32, name=f"result{b}", align_bytes=ROW)
                 nc.scalar.activation(result[:], y[b][:], ACT.Copy, scale=1.0 / 16.0)
                 queue = nc.sync if b == 0 else nc.scalar
                 queue.dma_start(out[0, b * P : (b + 1) * P, :], result[:])

@@ -32,7 +32,7 @@ ODD_SPLIT = T // 8 + 1
 RAW_BYTES = 4 * PACK * P
 KEY_BYTES = 2 * PAGE
 EARLY = 2
-VS_SPREAD = 1856
+VS_SPREAD = 2240
 ROW = 256
 KS_PIECES = ((0, PAGES - 1), (PAGES - 1, 1))
 SILU_AT = 512
@@ -41,7 +41,6 @@ KS_GOT_AT = 3 * RAW_BYTES - 64
 VW_AT = 3 * RAW_BYTES
 GOT2_AT = Q_AT[0, 1] + KEY_BYTES
 KS_AT = Q_AT[1, 0] + RAW_BYTES
-VS_AT = KS_AT + T
 KEYS_AT = {(1, 0): Q_AT[0, 0], (1, 1): Q_AT[0, 1], (2, 0): Q_AT[1, 0], (2, 1): SILU_AT + EARLY * RAW_BYTES}
 
 
@@ -55,16 +54,16 @@ def tile_attend_pkv4_silu_kernel(tc, qT, k_words, k_scales, v_words, v_scales, v
         voffs_sb = keep.tile([P, PAGES * DV // 16], U16, name="voffs_sb")
         nc.sync.dma_start(voffs_sb[:], voffs)
         vsc_pool = keep.tile([P, POOL_PAGES * DV // 4], I32, name="vsc_pool", align_bytes=ROW)
-        nc.scalar.dma_start(
+        nc.sync.dma_start(
             vsc_pool[VSC_ROW:P, :].rearrange("f (u e) -> f u e", u=POOL_PAGES),
             v_scales.bitcast(I32).rearrange("u f e -> f u e"),
         )
-        ks_pool = shared.tile([P, T // 4], I32, name="ks_pool", align_bytes=ROW, offset=KS_AT)
-        nc.sync.dma_start(ks_pool[KS_ROW : KS_ROW + 32, :], k_scales.bitcast(I32).rearrange("o (h a) t -> a (o h) t", h=2))
-        vs_pool = shared.tile([P, T], F32, name="vs_pool", align_bytes=ROW, offset=VS_AT)
-        nc.scalar.dma_start(vs_pool[VS_ROW:P, :], vs[0:1, :])
         offs_sb = keep.tile([P, N // 16], U16, name="offs_sb")
         nc.sync.dma_start(offs_sb[:], offs)
+        ks_pool = shared.tile([P, T // 4], I32, name="ks_pool", align_bytes=ROW, offset=KS_AT)
+        nc.sync.dma_start(ks_pool[KS_ROW : KS_ROW + 32, :], k_scales.bitcast(I32).rearrange("o f t -> f o t"))
+        vs_pool = keep.tile([P, T], F32, name="vs_pool", align_bytes=ROW)
+        nc.sync.dma_start(vs_pool[VS_ROW:P, :], vs[0:1, :])
         q_rows = qT[0].rearrange("(o p j) (b q) -> b o p j q", o=PASSES, j=PACK, b=QBLOCKS)
         q_raw = {}
 
@@ -118,8 +117,7 @@ def tile_attend_pkv4_silu_kernel(tc, qT, k_words, k_scales, v_words, v_scales, v
             )
         planes = shared.tile([P, PASSES * N // 4], I32, name="planes", align_bytes=ROW, offset=KS_AT)
         for c in (0, 2, 1, 3):
-            first = KS_ROW + 16 * (c % 2) + c // 2
-            nc.sync.dma_start(planes[32 * c : 32 * c + 4, :], ks_dealt[first : first + 15 : 2, :])
+            nc.sync.dma_start(planes[32 * c : 32 * c + 4, :], ks_dealt[KS_ROW + 8 * c : KS_ROW + 8 * c + 8, :])
         ks_plane = {}
         for g in range(PAGES):
             for o in range(PASSES):
@@ -148,7 +146,7 @@ def tile_attend_pkv4_silu_kernel(tc, qT, k_words, k_scales, v_words, v_scales, v
         q_codes = keep.tile([P, QBLOCKS * PASSES * P], U32, name="q_codes", align_bytes=64)
         q_scales = keep.tile([P, QBLOCKS * PASSES * P], U8, name="q_scales", align_bytes=64)
 
-        q_bf = shared.tile([P, QBLOCKS * PASSES * P * PACK], BF16, name="q_bf", align_bytes=64, offset=VS_AT)
+        q_bf = keep.tile([P, QBLOCKS * PASSES * P * PACK], BF16, name="q_bf", tag="q_bf", align_bytes=64)
 
         def cast_queries(b, o):
             at = (b * PASSES + o) * P * PACK
@@ -200,7 +198,7 @@ def tile_attend_pkv4_silu_kernel(tc, qT, k_words, k_scales, v_words, v_scales, v
         part_keys(2, 0, got2)
         quantise_queries(1, 1)
         part_keys(2, 1, got2)
-        vw_got = shared.tile([P, PAGES * DV], U32, name="vw_got", align_bytes=64, offset=VS_AT)
+        vw_got = keep.tile([P, PAGES * DV], U32, name="vw_got", tag="q_bf", align_bytes=64)
         nc.vector.tensor_copy(vw_got[:], vw_pool[:].bitcast(U32).indirect(voffs_sb[:]))
 
         vsc_words = keep.tile([P, PAGES * DV // 4], I32, name="vsc_words", tag="got0", align_bytes=64)

@@ -31,17 +31,23 @@ VSC_ROW = P - 16
 ODD_SPLIT = T // 8 + 1
 RAW_BYTES = 4 * PACK * P
 KEY_BYTES = 2 * PAGE
-EARLY = 2
+EARLY = PAGES
 VS_SPREAD = 2240
 ROW = 256
 KS_PIECES = ((0, PAGES - 1), (PAGES - 1, 1))
-SILU_AT = 512
-Q_AT = {(1, 1): 2 * RAW_BYTES, (0, 0): 5 * RAW_BYTES, (0, 1): 6 * RAW_BYTES, (1, 0): 7 * RAW_BYTES + KEY_BYTES}
-KS_GOT_AT = 3 * RAW_BYTES - 64
-VW_AT = 3 * RAW_BYTES
-GOT2_AT = Q_AT[0, 1] + KEY_BYTES
-KS_AT = Q_AT[1, 0] + RAW_BYTES
-KEYS_AT = {(1, 0): Q_AT[0, 0], (1, 1): Q_AT[0, 1], (2, 0): Q_AT[1, 0], (2, 1): SILU_AT + EARLY * RAW_BYTES}
+GOT2_AT = 2 * RAW_BYTES - KEY_BYTES // 2
+SILU_AT = GOT2_AT + RAW_BYTES
+LATE_Q_AT = SILU_AT + EARLY * RAW_BYTES - 2 * ROW
+KEYS_AT = {
+    (0, 1): 0,
+    (1, 0): RAW_BYTES - KEY_BYTES // 2,
+    (1, 1): RAW_BYTES + KEY_BYTES // 2,
+}
+VW_GOT_AT = LATE_Q_AT + 2 * ROW
+VSC_PLANE_AT = VW_GOT_AT + 4 * PAGES * DV
+KS_GOT_AT = LATE_Q_AT + PASSES * RAW_BYTES - 64
+VW_AT = LATE_Q_AT + PASSES * RAW_BYTES + ROW
+KS_AT = VW_AT + 4 * POOL_PAGES * DV
 
 
 def tile_attend_pkv4_silu_kernel(tc, qT, k_words, k_scales, v_words, v_scales, vs, offs, voffs, out):
@@ -67,17 +73,12 @@ def tile_attend_pkv4_silu_kernel(tc, qT, k_words, k_scales, v_words, v_scales, v
         q_rows = qT[0].rearrange("(o p j) (b q) -> b o p j q", o=PASSES, j=PACK, b=QBLOCKS)
         q_raw = {}
 
-        def load_queries(b, o, pieces=1):
-            q_raw[b, o] = shared.tile([P, PACK, P], F32, name=f"q_raw{b}_{o}", align_bytes=ROW, offset=Q_AT[b, o])
-            rows = PACK // pieces
-            for j in range(0, PACK, rows):
-                nc.sync.dma_start(q_raw[b, o][:, j : j + rows, :], q_rows[b, o][:, j : j + rows, :])
 
         kw_pool = keep.tile([P, T], I32, name="kw_pool", align_bytes=ROW)
         nc.sync.dma_start(kw_pool[:], k_words[0].rearrange("g t b -> g (t b)").bitcast(I32))
-        load_queries(0, 0)
-        load_queries(0, 1)
-        load_queries(1, 0, pieces=2)
+        for o in range(PASSES):
+            q_raw[0, o] = shared.tile([P, PACK, P], F32, name=f"q_raw{o}", align_bytes=ROW, offset=o * RAW_BYTES)[:]
+            nc.sync.dma_start(q_raw[0, o], q_rows[0, o])
 
         warm_in = keep.tile([P, 1], F32, name="warm_in")
         nc.vector.memset(warm_in[:], 0.0)
@@ -122,7 +123,10 @@ def tile_attend_pkv4_silu_kernel(tc, qT, k_words, k_scales, v_words, v_scales, v
         for g in range(PAGES):
             for o in range(PASSES):
                 ks_plane[g, o] = planes[:].bitcast(U8)[:, o * N + g * PAGE : o * N + (g + 1) * PAGE]
-        load_queries(1, 1)
+        late_q = shared.tile([P, PASSES, PACK, P], F32, name="late_q", align_bytes=ROW, offset=LATE_Q_AT)
+        for o in range(PASSES):
+            q_raw[1, o] = late_q[:, o]
+            nc.sync.dma_start(q_raw[1, o], q_rows[1, o])
         vw_pool = shared.tile([P, POOL_PAGES * DV], I32, name="vw_pool", align_bytes=ROW, offset=VW_AT)
         nc.sync.dma_start(
             vw_pool[:].rearrange("g (u e) -> g u e", u=POOL_PAGES),
@@ -146,13 +150,13 @@ def tile_attend_pkv4_silu_kernel(tc, qT, k_words, k_scales, v_words, v_scales, v
         q_codes = keep.tile([P, QBLOCKS * PASSES * P], U32, name="q_codes", align_bytes=64)
         q_scales = keep.tile([P, QBLOCKS * PASSES * P], U8, name="q_scales", align_bytes=64)
 
-        q_bf = keep.tile([P, QBLOCKS * PASSES * P * PACK], BF16, name="q_bf", tag="q_bf", align_bytes=64)
+        q_bf = keep.tile([P, QBLOCKS * PASSES * P * PACK], BF16, name="q_bf", align_bytes=64)
 
         def cast_queries(b, o):
             at = (b * PASSES + o) * P * PACK
             nc.scalar.copy(
                 q_bf[:, at : at + P * PACK].rearrange("p (c i j) -> p c j i", i=4, j=PACK),
-                q_raw[b, o][:].rearrange("p j (c i) -> p c j i", i=4),
+                q_raw[b, o].rearrange("p j (c i) -> p c j i", i=4),
             )
 
         def quantise_queries(b, o):
@@ -188,25 +192,25 @@ def tile_attend_pkv4_silu_kernel(tc, qT, k_words, k_scales, v_words, v_scales, v
         got0 = gather_keys(0)
         got1 = gather_keys(1)
         part_keys(0, 0, got0)
-        part_keys(0, 1, got0)
         quantise_queries(0, 0)
-        part_keys(1, 0, got1)
+        part_keys(0, 1, got0)
         quantise_queries(0, 1)
+        part_keys(1, 0, got1)
         got2 = gather_keys(2)
         part_keys(1, 1, got1)
-        quantise_queries(1, 0)
         part_keys(2, 0, got2)
-        quantise_queries(1, 1)
         part_keys(2, 1, got2)
-        vw_got = keep.tile([P, PAGES * DV], U32, name="vw_got", tag="q_bf", align_bytes=64)
+        quantise_queries(1, 0)
+        quantise_queries(1, 1)
+        vw_got = shared.tile([P, PAGES * DV], U32, name="vw_got", align_bytes=64, offset=VW_GOT_AT)
         nc.vector.tensor_copy(vw_got[:], vw_pool[:].bitcast(U32).indirect(voffs_sb[:]))
 
-        vsc_words = keep.tile([P, PAGES * DV // 4], I32, name="vsc_words", tag="got0", align_bytes=64)
+        vsc_words = shared.tile([P, PAGES * DV // 4], I32, name="vsc_words", align_bytes=ROW, offset=VSC_PLANE_AT)
         vsc_plane = vsc_words[:].bitcast(U8)
         for c in range(4):
             nc.sync.dma_start(vsc_words[32 * c : 32 * c + 4, :], vsc_got[:].bitcast(I32)[VSC_ROW + 4 * c : VSC_ROW + 4 * c + 4, :])
 
-        chunks = [(0, 0), (1, 0), (0, 1), (2, 0), (1, 1), (2, 1)]
+        chunks = [(g, b) for b in range(QBLOCKS) for g in range(PAGES)]
         score = {}
         for g, b in chunks:
             score[g, b] = psum.tile([P, PACK, P], F32, name=f"score{g}_{b}", tag=f"score{g}_{b}")
@@ -234,7 +238,7 @@ def tile_attend_pkv4_silu_kernel(tc, qT, k_words, k_scales, v_words, v_scales, v
                 silu[g, b] = keep.tile([P, P, PACK], F32, name=f"silu{g}_{b}", align_bytes=64)[:]
             nc.scalar.activation(silu[g, b], score[g, b][:].rearrange("p t q -> p q t"), ACT.Silu)
 
-        y = [psum.tile([P, DV], F32, name=f"y{b}", tag=f"score{PAGES - 1}_{b}") for b in range(QBLOCKS)]
+        y = [psum.tile([P, DV], F32, name=f"y{b}", tag=f"score{PAGES - QBLOCKS + b}_{QBLOCKS - 1}") for b in range(QBLOCKS)]
 
         def scale(g, b):
             w_bf = keep.tile([P, P, PACK], BF16, name=f"w_bf{g}_{b}", align_bytes=64)

from contextlib import ExitStack

import concourse.mybir as mybir
from concourse.masks import make_identity

N, T, D, DV, NQ = 1536, 4096, 1024, 128, 256
PAGE = 512
FLOPS = 2 * NQ * D * N + 2 * NQ * N * DV

F32 = mybir.dt.float32
BF16 = mybir.dt.bfloat16
I32 = mybir.dt.int32
U32 = mybir.dt.uint32
U16 = mybir.dt.uint16
U8 = mybir.dt.uint8
FP8X4 = mybir.dt.float8_e4m3fn_x4
FP4X4 = mybir.dt.float4_e2m1fn_x4
ACT = mybir.ActivationFunctionType
MULT = mybir.AluOpType.mult

P = 128
PACK = 4
PASSES = D // (P * PACK)
PAGES = N // PAGE
POOL_PAGES = T // PAGE
QBLOCKS = NQ // P
LIST_COLS = PAGE // 16
VS_ROW = P - 1
KS_ROW = 32
VSC_ROW = P - 16
ODD_SPLIT = T // 8 + 1
RAW_BYTES = 4 * PACK * P
KEY_BYTES = 2 * PAGE
EARLY = PAGES
VS_SPREAD = 2240
ROW = 256
KS_PIECES = ((0, PAGES - 1), (PAGES - 1, 1))
GOT2_AT = 2 * RAW_BYTES - KEY_BYTES // 2
SILU_AT = GOT2_AT + RAW_BYTES
LATE_Q_AT = SILU_AT + EARLY * RAW_BYTES - 2 * ROW
KEYS_AT = {
    (0, 1): 0,
    (1, 0): RAW_BYTES - KEY_BYTES // 2,
    (1, 1): RAW_BYTES + KEY_BYTES // 2,
}
VW_GOT_AT = LATE_Q_AT + 2 * ROW
VSC_PLANE_AT = VW_GOT_AT + 4 * PAGES * DV
KS_GOT_AT = LATE_Q_AT + PASSES * RAW_BYTES - 64
VW_AT = LATE_Q_AT + PASSES * RAW_BYTES + ROW
KS_AT = VW_AT + 4 * POOL_PAGES * DV


def tile_attend_pkv4_silu_kernel(tc, qT, k_words, k_scales, v_words, v_scales, vs, offs, voffs, out):
    nc = tc.nc
    with ExitStack() as ctx:
        keep = ctx.enter_context(tc.tile_pool(name="keep", bufs=1))
        shared = ctx.enter_context(tc.tile_pool(name="shared", bufs=1))
        psum = ctx.enter_context(tc.psum_pool(name="psum", bufs=1))

        voffs_sb = keep.tile([P, PAGES * DV // 16], U16, name="voffs_sb")
        nc.sync.dma_start(voffs_sb[:], voffs)
        vsc_pool = keep.tile([P, POOL_PAGES * DV // 4], I32, name="vsc_pool", align_bytes=ROW)
        nc.sync.dma_start(
            vsc_pool[VSC_ROW:P, :].rearrange("f (u e) -> f u e", u=POOL_PAGES),
            v_scales.bitcast(I32).rearrange("u f e -> f u e"),
        )
        offs_sb = keep.tile([P, N // 16], U16, name="offs_sb")
        nc.sync.dma_start(offs_sb[:], offs)
        ks_pool = shared.tile([P, T // 4], I32, name="ks_pool", align_bytes=ROW, offset=KS_AT)
        nc.sync.dma_start(ks_pool[KS_ROW : KS_ROW + 32, :], k_scales.bitcast(I32).rearrange("o f t -> f o t"))
        vs_pool = keep.tile([P, T], F32, name="vs_pool", align_bytes=ROW)
        nc.sync.dma_start(vs_pool[VS_ROW:P, :], vs[0:1, :])
        q_rows = qT[0].rearrange("(o p j) (b q) -> b o p j q", o=PASSES, j=PACK, b=QBLOCKS)
        q_raw = {}


        kw_pool = keep.tile([P, T], I32, name="kw_pool", align_bytes=ROW)
        nc.sync.dma_start(kw_pool[:], k_words[0].rearrange("g t b -> g (t b)").bitcast(I32))
        for o in range(PASSES):
            q_raw[0, o] = shared.tile([P, PACK, P], F32, name=f"q_raw{o}", align_bytes=ROW, offset=o * RAW_BYTES)[:]
            nc.sync.dma_start(q_raw[0, o], q_rows[0, o])

        warm_in = keep.tile([P, 1], F32, name="warm_in")
        nc.vector.memset(warm_in[:], 0.0)
        nc.vector.memset(vs_pool[0:VS_ROW, 0:1].bitcast(I32), 0)
        for cols in (slice(0, ODD_SPLIT), slice(ODD_SPLIT, T // 4)):
            nc.vector.memset(ks_pool[KS_ROW + 32 : P, cols], 0)

        ident = keep.tile([P, P], F32, name="ident", align_bytes=64)
        nc.gpsimd.memset(ident[:], 0.0)
        nc.gpsimd.memset(vsc_pool[0:VSC_ROW, :], 0)
        nc.gpsimd.memset(ks_pool[0:KS_ROW, :], 0)
        make_identity(nc, ident[:], nomemset=True)
        nc.gpsimd.memset(vs_pool[0:VS_ROW, VS_SPREAD:T].bitcast(I32), 0)
        warmed = keep.tile([P, 1], F32, name="warmed")
        nc.scalar.activation(warmed[:], warm_in[:], ACT.Silu)
        nc.scalar.activation(
            vs_pool[0:VS_ROW, 1:VS_SPREAD], vs_pool[0:VS_ROW, 0:1].to_broadcast([VS_ROW, VS_SPREAD - 1]), ACT.Copy
        )

        vsc_got = keep.tile([P, PAGES * DV], U8, name="vsc_got", align_bytes=64)
        nc.vector.tensor_copy(vsc_got[:], vsc_pool[:].bitcast(U8).indirect(voffs_sb[:]))
        ks_got = []
        for first, count in KS_PIECES:
            if first == 0:
                got = keep.tile([P, count * PAGE], U8, name=f"ks_got{first}", align_bytes=64)
            else:
                got = shared.tile([P, count * PAGE], U8, name=f"ks_got{first}", align_bytes=64, offset=KS_GOT_AT)
            listed = offs_sb[:, first * LIST_COLS : (first + count) * LIST_COLS]
            nc.vector.tensor_copy(got[:], ks_pool[:].bitcast(U8).indirect(listed))
            ks_got.append(got)
        ks_dealt = keep.tile([P, N // 4], I32, name="ks_dealt", align_bytes=ROW)
        for (first, count), got in zip(KS_PIECES, ks_got):
            dealt = ks_dealt[:].bitcast(U8)[:, first * PAGE : (first + count) * PAGE]
            nc.vector.tensor_copy(
                dealt.rearrange("p (g h t s) -> p h g t s", g=count, h=2, t=PACK // 2),
                got[:].rearrange("p (g s h t) -> p h g t s", g=count, h=2, t=PACK // 2),
            )
        planes = shared.tile([P, PASSES * N // 4], I32, name="planes", align_bytes=ROW, offset=KS_AT)
        for c in (0, 2, 1, 3):
            nc.sync.dma_start(planes[32 * c : 32 * c + 4, :], ks_dealt[KS_ROW + 8 * c : KS_ROW + 8 * c + 8, :])
        ks_plane = {}
        for g in range(PAGES):
            for o in range(PASSES):
                ks_plane[g, o] = planes[:].bitcast(U8)[:, o * N + g * PAGE : o * N + (g + 1) * PAGE]
        late_q = shared.tile([P, PASSES, PACK, P], F32, name="late_q", align_bytes=ROW, offset=LATE_Q_AT)
        for o in range(PASSES):
            q_raw[1, o] = late_q[:, o]
            nc.sync.dma_start(q_raw[1, o], q_rows[1, o])
        vw_pool = shared.tile([P, POOL_PAGES * DV], I32, name="vw_pool", align_bytes=ROW, offset=VW_AT)
        nc.sync.dma_start(
            vw_pool[:].rearrange("g (u e) -> g u e", u=POOL_PAGES),
            v_words.rearrange("u g e r -> g u (e r)").bitcast(I32),
        )

        vs_got = []
        for g in range(PAGES):
            got = keep.tile([P, PAGE], F32, name=f"vs_got{g}", align_bytes=64)
            nc.scalar.activation(got[:], vs_pool[:].indirect(offs_sb[:, g * LIST_COLS : (g + 1) * LIST_COLS]), ACT.Copy)
            vs_got.append(got)

        vs_bank = psum.tile([P, PAGE], F32, name="vs_bank")
        vs_col = []
        for g in range(PAGES):
            first = 2 * PACK * (PAGES - 1 - g)
            for t in reversed(range(PACK)):
                nc.tensor.transpose(vs_bank[:, first + 2 * t : first + 2 * t + P], vs_got[g][:, t:PAGE:PACK], ident[:])
            vs_col.append(vs_bank[:, first + VS_ROW : first + VS_ROW + 2 * PACK : 2])

        q_codes = keep.tile([P, QBLOCKS * PASSES * P], U32, name="q_codes", align_bytes=64)
        q_scales = keep.tile([P, QBLOCKS * PASSES * P], U8, name="q_scales", align_bytes=64)

        q_bf = keep.tile([P, QBLOCKS * PASSES * P * PACK], BF16, name="q_bf", align_bytes=64)

        def cast_queries(b, o):
            at = (b * PASSES + o) * P * PACK
            nc.scalar.copy(
                q_bf[:, at : at + P * PACK].rearrange("p (c i j) -> p c j i", i=4, j=PACK),
                q_raw[b, o].rearrange("p j (c i) -> p c j i", i=4),
            )

        def quantise_queries(b, o):
            at = (b * PASSES + o) * P
            nc.vector.quantize_mx(
                out=q_codes[:, at : at + P].bitcast(FP8X4),
                scales=q_scales[:, at : at + P],
                in_=q_bf[:, at * PACK : (at + P) * PACK],
            )

        def gather_keys(g):
            if g == PAGES - 1:
                kw_got = shared.tile([P, PAGE], U32, name=f"kw_got{g}", align_bytes=64, offset=GOT2_AT)
            else:
                kw_got = keep.tile([P, PAGE], U32, name=f"kw_got{g}", tag=f"got{g}", align_bytes=64)
            nc.vector.tensor_copy(kw_got[:], kw_pool[:].bitcast(U32).indirect(offs_sb[:, g * LIST_COLS : (g + 1) * LIST_COLS]))
            return kw_got

        keys = {}

        def part_keys(g, o, kw_got):
            if (g, o) in KEYS_AT:
                tile = shared.tile([P, KEY_BYTES], U8, name=f"keys{g}_{o}", align_bytes=64, offset=KEYS_AT[g, o])
            else:
                tile = keep.tile([P, KEY_BYTES], U8, name=f"keys{g}_{o}", align_bytes=64)
            halves = kw_got[:].bitcast(U16).rearrange("p (c i t o) -> p o c t i", i=4, t=PACK, o=PASSES)
            nc.vector.tensor_copy(tile[:].bitcast(U16).rearrange("p (t c i) -> p c t i", t=PACK, i=4), halves[:, o])
            keys[g, o] = tile

        for b in range(QBLOCKS):
            for o in range(PASSES):
                cast_queries(b, o)
        got0 = gather_keys(0)
        got1 = gather_keys(1)
        part_keys(0, 0, got0)
        quantise_queries(0, 0)
        part_keys(0, 1, got0)
        quantise_queries(0, 1)
        part_keys(1, 0, got1)
        got2 = gather_keys(2)
        part_keys(1, 1, got1)
        part_keys(2, 0, got2)
        part_keys(2, 1, got2)
        quantise_queries(1, 0)
        quantise_queries(1, 1)
        vw_got = shared.tile([P, PAGES * DV], U32, name="vw_got", align_bytes=64, offset=VW_GOT_AT)
        nc.vector.tensor_copy(vw_got[:], vw_pool[:].bitcast(U32).indirect(voffs_sb[:]))

        vsc_words = shared.tile([P, PAGES * DV // 4], I32, name="vsc_words", align_bytes=ROW, offset=VSC_PLANE_AT)
        vsc_plane = vsc_words[:].bitcast(U8)
        for c in range(4):
            nc.sync.dma_start(vsc_words[32 * c : 32 * c + 4, :], vsc_got[:].bitcast(I32)[VSC_ROW + 4 * c : VSC_ROW + 4 * c + 4, :])

        chunks = [(g, b) for b in range(QBLOCKS) for g in range(PAGES)]
        score = {}
        for g, b in chunks:
            score[g, b] = psum.tile([P, PACK, P], F32, name=f"score{g}_{b}", tag=f"score{g}_{b}")

        def score_pass(g, b, o):
            for t in range(PACK):
                nc.tensor.matmul_mx(
                    out=score[g, b][:, t, :],
                    lhsT=keys[g, o][:, 2 * P * t : 2 * P * (t + 1)].bitcast(FP4X4),
                    lhsT_scale=ks_plane[g, o][:, P * t : P * (t + 1)],
                    rhs=q_codes[:, (b * PASSES + o) * P : (b * PASSES + o + 1) * P].bitcast(FP8X4),
                    rhs_scale=q_scales[:, (b * PASSES + o) * P : (b * PASSES + o + 1) * P],
                    start=(o == 0 and t == 0),
                    stop=(o == PASSES - 1 and t == PACK - 1),
                )

        silu = {}
        early_silu = shared.tile([P, EARLY, P, PACK], F32, name="early_silu", align_bytes=64, offset=SILU_AT)
        for n, (g, b) in enumerate(chunks):
            for o in range(PASSES):
                score_pass(g, b, o)
            if n < EARLY:
                silu[g, b] = early_silu[:, n]
            else:
                silu[g, b] = keep.tile([P, P, PACK], F32, name=f"silu{g}_{b}", align_bytes=64)[:]
            nc.scalar.activation(silu[g, b], score[g, b][:].rearrange("p t q -> p q t"), ACT.Silu)

        y = [psum.tile([P, DV], F32, name=f"y{b}", tag=f"score{PAGES - QBLOCKS + b}_{QBLOCKS - 1}") for b in range(QBLOCKS)]

        def scale(g, b):
            w_bf = keep.tile([P, P, PACK], BF16, name=f"w_bf{g}_{b}", align_bytes=64)
            nc.vector.tensor_tensor(w_bf[:], silu[g, b], vs_col[g].unsqueeze(1).to_broadcast([P, P, PACK]), MULT)
            return w_bf

        def quantise_weights(g, b, w_bf):
            w_codes = keep.tile([P, P], U32, name=f"w_codes{g}_{b}", align_bytes=64)
            w_scales = keep.tile([P, P], U8, name=f"w_scales{g}_{b}", align_bytes=64)
            nc.vector.quantize_mx(
                out=w_codes[:].bitcast(FP8X4), scales=w_scales[:], in_=w_bf[:].rearrange("p q t -> p (q t)")
            )
            return g, b, w_codes, w_scales

        def multiply(g, b, w_codes, w_scales):
            nc.tensor.matmul_mx(
                out=y[b][:],
                lhsT=w_codes[:].bitcast(FP8X4),
                lhsT_scale=w_scales[:],
                rhs=vw_got[:, g * DV : (g + 1) * DV].bitcast(FP8X4),
                rhs_scale=vsc_plane[:, g * DV : (g + 1) * DV],
                start=(g == 0),
                stop=(g == PAGES - 1),
            )
            if g == PAGES - 1:
                result = keep.tile([P, DV], F32, name=f"result{b}", align_bytes=ROW)
                nc.scalar.activation(result[:], y[b][:], ACT.Copy, scale=1.0 / 16.0)
                queue = nc.sync if b == 0 else nc.scalar
                queue.dma_start(out[0, b * P : (b + 1) * P, :], result[:])

        pending = None
        quantised = []
        for g, b in chunks:
            w_bf = scale(g, b)
            if pending is not None:
                quantised.append(quantise_weights(*pending))
            pending = (g, b, w_bf)
        quantised.append(quantise_weights(*pending))
        for item in quantised:
            multiply(*item)
